import numpy as np
import ml_dtypes


def mxq(x, axis, fmt="e4m3"):
    dtype, down = {"e4m3": (ml_dtypes.float8_e4m3fn, 7), "e5m2": (ml_dtypes.float8_e5m2, 14)}[fmt]
    v = np.moveaxis(np.asarray(x, np.float32).astype(ml_dtypes.bfloat16).astype(np.float64), axis, -1)
    blocks = v.reshape(v.shape[:-1] + (-1, 32))
    amax = np.abs(blocks).max(-1, keepdims=True)
    byte = np.maximum(np.where(amax > 0, np.frexp(amax)[1] - 1 + 127, 0) - down, 1)
    scale = np.exp2(byte - 127.0)
    codes = (blocks / scale).astype(np.float32).astype(dtype).astype(np.float64)
    return np.moveaxis((codes * scale).reshape(v.shape), -1, axis)


WIDE = False


def mx_kscale(k):
    if not WIDE:
        return np.ones(k)
    levels = np.array([10, -10, 5, -5, 0])
    if k % 512:
        return np.exp2(np.random.permutation(np.resize(levels, k // 32))).repeat(32)
    a = np.empty((k // 512, 16))
    for p in range(k // 512):
        a[p, :8] = np.random.permutation(np.resize(levels, 8))
        for g in range(8):
            far = levels[np.abs(levels - a[p, g]) >= 10]
            a[p, g + 8] = far[np.random.randint(len(far))]
    return np.exp2(a.ravel()).repeat(32)


def f64(x):
    return np.asarray(x).astype(np.float64)


def striped(idx):
    return np.tile(np.asarray(idx).reshape(-1, 16).T, (8, 1)).astype(np.uint16)


def unstriped(offs):
    return offs[:16].T.reshape(-1).astype(np.int64)


B, N, T, D, DV, NQ = 1, 512, 2048, 512, 256, 128


def setup_inputs():
    n = np.random.standard_normal
    idx = np.random.permutation(T)[:B * N]
    s = mx_kscale(D)[:, None]
    u = np.ones(T)
    u[idx] = mx_kscale(B * N)
    r = np.random.uniform(0.5, 2.0, T)
    long = np.random.uniform(0.9, 1.1, T)
    k = n((D, T)) / s * long
    v = n((DV, T)) / (u * r)
    return {
        "qT": (n((B, D, NQ)) * s * (0.80 / np.sqrt(D))).astype(np.float32),
        "kT": k.astype(np.float32),
        "vT": v.astype(np.float32),
        "vs": np.tile(u * r, (128, 1)).astype(np.float32),
        "kb": np.tile(-0.5 * np.sum(np.square(k * s), 0) * (0.80 / np.sqrt(D)), (128, 1)).astype(np.float32),
        "og": n((B, NQ, DV)).astype(np.float32),
        "offs": striped(idx),
    }


def reference(qT, kT, vT, vs, kb, og, offs):
    idx = unstriped(offs)
    k = f64(kT)
    v = f64(vT)
    pick = lambda x: x[:, idx].reshape(x.shape[0], B, N).transpose(1, 0, 2)
    q = f64(qT)
    score = mxq(q, 1, "e4m3").transpose(0, 2, 1) @ mxq(pick(k), 1, "e4m3")
    score = score + pick(f64(kb))[:, :1, :]
    m = score.max(-1, keepdims=True)
    p = np.exp(score - m)
    total = p.sum(-1, keepdims=True)
    w = p * pick(f64(vs))[:, :1, :]
    y = mxq(w, 2, "e4m3") @ mxq(pick(v).transpose(0, 2, 1), 1, "e4m3")
    y = y / total
    y = y / (1.0 + np.exp(-f64(og)))
    return y

@@ -1,0 +1,232 @@
+from contextlib import ExitStack
+
+import concourse.mybir as mybir
+from concourse.masks import make_identity
+
+F32 = mybir.dt.float32
+BF16 = mybir.dt.bfloat16
+U32 = mybir.dt.uint32
+U16 = mybir.dt.uint16
+U8 = mybir.dt.uint8
+FP8X4 = mybir.dt.float8_e4m3fn_x4
+ADD = mybir.AluOpType.add
+SUB = mybir.AluOpType.subtract
+MULT = mybir.AluOpType.mult
+MIN = mybir.AluOpType.min
+ACT = mybir.ActivationFunctionType
+AXIS_X = mybir.AxisListType.X
+
+P = 128
+PACK = 4
+N = 512
+T = 2048
+D = 512
+DV = 256
+NQ = 128
+
+FLOPS = 2 * NQ * N * D + 2 * NQ * N * DV
+BYTES = 4 * (D * NQ + D * T + DV * T + 2 * T + 2 * NQ * DV) + 2 * P * (N // 16)
+
+
+def tile_attend_x_norm_gate_topk_kernel(tc, qT, kT, vT, vs, kb, og, offs, out):
+    nc = tc.nc
+    with ExitStack() as ctx:
+        keep = ctx.enter_context(tc.tile_pool(name="keep", bufs=1))
+        psum = ctx.enter_context(tc.psum_pool(name="psum", bufs=1))
+
+        offsets = keep.tile([P, N // 16], U16, name="offsets")
+        q_raw = keep.tile([P, PACK, NQ], F32, name="q_raw")
+        k_pool = [keep.tile([P, T], F32, name="k_pool%d" % t) for t in range(PACK)]
+        v_pool = [keep.tile([P, T], F32, name="v_pool%d" % b) for b in range(2)]
+        kb_pool = keep.tile([P, T], F32, name="kb_pool")
+        vs_pool = keep.tile([P, T], F32, name="vs_pool")
+        gate_raw = keep.tile([P, DV], F32, name="gate_raw")
+        warm = keep.tile([P, 1], F32, name="warm")
+        ident = keep.tile([P, P], F32, name="ident")
+
+        nc.vector.memset(warm[:], 0.0)
+        nc.vector.memset(kb_pool[:], 0.0)
+        nc.vector.memset(vs_pool[:], 0.0)
+        nc.sync.dma_start(offsets[:], offs)
+        k_rows = kT.rearrange("(p t) n -> p t n", t=PACK)
+        for t in range(PACK):
+            nc.sync.dma_start(out=k_pool[t][:], in_=k_rows[:, t, :])
+            if t == 0:
+                nc.sync.dma_start(out=kb_pool[0:1, :], in_=kb[0:1, :])
+            if t == 1:
+                nc.sync.dma_start(out=vs_pool[0:1, :], in_=vs[0:1, :])
+        nc.sync.dma_start(out=q_raw[:], in_=qT.rearrange("b (p t) q -> p (b t) q", t=PACK))
+        for b in range(2):
+            nc.sync.dma_start(out=v_pool[b][:], in_=vT[b * P : (b + 1) * P, :])
+        nc.sync.dma_start(out=gate_raw[:], in_=og.rearrange("b q e -> (b q) e"))
+        make_identity(nc, ident[:])
+        warm_out = keep.tile([P, 1], F32, name="warm_out")
+        nc.scalar.activation(warm_out[:], warm[:], ACT.Exp)
+
+        k_grouped = keep.tile([P, N, PACK], BF16, name="k_grouped", align_bytes=64)
+        idle_bank = psum.tile([P, 4, P], F32, name="idle_bank", tag="bank_idle")
+
+        def keep_clock(pool, count):
+            for c in range(count):
+                nc.tensor.transpose(idle_bank[:, c % 4, :], pool[:, c * P : (c + 1) * P], ident[:])
+
+        nc.vector.tensor_copy(k_grouped[:, :, 0], k_pool[0][:].indirect(offsets[:]))
+        kb_row = keep.tile([P, N], F32, name="kb_row")
+        nc.vector.tensor_copy(kb_row[:], kb_pool[:].indirect(offsets[:]))
+        kb_turned = psum.tile([P, 4, P], F32, name="kb_turned", tag="bank_a")
+        for c in range(4):
+            nc.tensor.transpose(kb_turned[:, c, :], kb_row[:, c * P : (c + 1) * P], ident[:])
+        kb_cols = keep.tile([P, 4], F32, name="kb_cols")
+        nc.scalar.copy(kb_cols[:], kb_turned[:, :, 0])
+        kb_spread = psum.tile([P, 4, P], F32, name="kb_spread", tag="bank_b")
+        for c in range(4):
+            nc.tensor.transpose(kb_spread[:, c, :], kb_cols[:, c : c + 1].to_broadcast([P, P]), ident[:])
+        neg_kb = keep.tile([P, N], F32, name="neg_kb")
+        nc.scalar.activation(neg_kb[:], kb_spread[:].rearrange("p c q -> p (c q)"), ACT.Copy, scale=-1.0)
+
+        nc.vector.tensor_copy(k_grouped[:, :, 1], k_pool[1][:].indirect(offsets[:]))
+        vs_row = keep.tile([P, N], F32, name="vs_row")
+        nc.vector.tensor_copy(vs_row[:], vs_pool[:].indirect(offsets[:]))
+        vs_turned = psum.tile([P, PACK, P], F32, name="vs_turned", tag="bank_a")
+        for t in range(PACK):
+            nc.tensor.transpose(vs_turned[:, t, :], vs_row[:, t:N:PACK], ident[:])
+        vs_cols = keep.tile([P, PACK], F32, name="vs_cols")
+        nc.scalar.copy(vs_cols[:], vs_turned[:, :, 0])
+
+        nc.vector.tensor_copy(k_grouped[:, :, 2], k_pool[2][:].indirect(offsets[:]))
+        nc.vector.tensor_copy(k_grouped[:, :, 3], k_pool[3][:].indirect(offsets[:]))
+        q_grouped = keep.tile([P, NQ, PACK], BF16, name="q_grouped", align_bytes=64)
+        q_codes = keep.tile([P, NQ], U32, name="q_codes", align_bytes=64)
+        q_scales = keep.tile([P, NQ], U8, name="q_scales", align_bytes=64)
+        nc.scalar.copy(q_grouped[:], q_raw[:].rearrange("p t q -> p q t"))
+        nc.vector.quantize_mx(
+            out=q_codes[:].bitcast(FP8X4), scales=q_scales[:], in_=q_grouped[:].rearrange("p q t -> p (q t)")
+        )
+
+        keep_clock(k_pool[2], 14)
+        keep_clock(k_pool[3], 14)
+        k_codes = keep.tile([P, N], U32, name="k_codes", align_bytes=64)
+        k_scales = keep.tile([P, N], U8, name="k_scales", align_bytes=64)
+        k_flat = k_grouped[:].rearrange("p n t -> p (n t)")
+        half = N // 2
+        for h in range(2):
+            nc.vector.quantize_mx(
+                out=k_codes[:, h * half : (h + 1) * half].bitcast(FP8X4),
+                scales=k_scales[:, h * half : (h + 1) * half],
+                in_=k_flat[:, h * half * PACK : (h + 1) * half * PACK],
+            )
+        scores = [psum.tile([P, half], F32, name="scores%d" % h, tag="bank_s%d" % h) for h in range(2)]
+        neg_s = keep.tile([P, N], F32, name="neg_s")
+        for h in range(2):
+            cols = slice(h * half, (h + 1) * half)
+            nc.tensor.matmul_mx(
+                out=scores[h][:],
+                lhsT=q_codes[:].bitcast(FP8X4),
+                lhsT_scale=q_scales[:],
+                rhs=k_codes[:, cols].bitcast(FP8X4),
+                rhs_scale=k_scales[:, cols],
+                start=True,
+                stop=True,
+            )
+        v_words = []
+        v_grouped = []
+        v_codes = keep.tile([P, DV], U32, name="v_codes", align_bytes=64)
+        v_scales = keep.tile([P, DV], U8, name="v_scales", align_bytes=64)
+
+        v_cast = keep.tile([P, T], BF16, name="v_cast")
+
+        def gather_values(b):
+            words = keep.tile([P, 2, P, 2], BF16, name="v_words%d" % b)
+            columns = words[:].rearrange("e u s r -> e s u r")
+            if b == 0:
+                nc.scalar.activation(columns, v_cast[:].indirect(offsets[:]), ACT.Copy)
+            else:
+                nc.vector.tensor_copy(columns, v_pool[b][:].indirect(offsets[:]))
+            v_words.append(words)
+
+        def turn_values(b):
+            words = v_words[b][:].rearrange("e u s r -> e (u s r)").bitcast(F32)
+            turned = psum.tile([P, 2, P], F32, name="v_turned%d" % b, tag="bank_v%d" % b)
+            for u in range(2):
+                nc.tensor.transpose(turned[:, u, :], words[:, u * P : (u + 1) * P], ident[:])
+            grouped = keep.tile([P, P * PACK], BF16, name="v_grouped%d" % b, align_bytes=64)
+            nc.scalar.copy(
+                grouped[:].bitcast(F32).rearrange("s (e u) -> s e u", u=2), turned[:].rearrange("s u e -> s e u")
+            )
+            v_grouped.append(grouped)
+
+        def quantize_values(b):
+            cols = slice(b * P, (b + 1) * P)
+            nc.vector.quantize_mx(
+                out=v_codes[:, cols].bitcast(FP8X4), scales=v_scales[:, cols], in_=v_grouped[b][:]
+            )
+
+        keep_clock(v_pool[0], 10)
+        nc.vector.tensor_copy(v_cast[:, T // 2 :], v_pool[0][:, T // 2 :])
+        nc.scalar.activation(v_cast[:, : T // 2], v_pool[0][:, : T // 2], ACT.Copy)
+        gather_values(0)
+        keep_clock(v_pool[1], 8)
+        for h in range(2):
+            cols = slice(h * half, (h + 1) * half)
+            nc.vector.tensor_tensor(neg_s[:, cols], neg_kb[:, cols], scores[h][:], SUB)
+        neg_m = keep.tile([P, 1], F32, name="neg_m")
+        nc.vector.tensor_reduce(neg_m[:], neg_s[:], AXIS_X, MIN)
+
+        p = keep.tile([P, PACK, P], F32, name="p")
+        total = keep.tile([P, 1], F32, name="total")
+        nc.scalar.activation(
+            p[:].rearrange("q t s -> q s t"),
+            neg_s[:].rearrange("q (s t) -> q s t", t=PACK),
+            ACT.Exp,
+            bias=neg_m[:],
+            scale=-1.0,
+            accum_out=total[:],
+        )
+        p_turned = psum.tile([P, PACK, NQ], F32, name="p_turned", tag="bank_p")
+        for t in range(PACK):
+            nc.tensor.transpose(p_turned[:, t, :], p[:, t, :], ident[:])
+        turn_values(0)
+        gather_values(1)
+        quantize_values(0)
+        w = keep.tile([P, NQ, PACK], BF16, name="w", align_bytes=64)
+        w_codes = keep.tile([P, NQ], U32, name="w_codes", align_bytes=64)
+        w_scales = keep.tile([P, NQ], U8, name="w_scales", align_bytes=64)
+        nc.vector.tensor_tensor(
+            w[:],
+            p_turned[:].rearrange("s t q -> s q t"),
+            vs_cols[:].unsqueeze(1).to_broadcast([P, NQ, PACK]),
+            MULT,
+        )
+        turn_values(1)
+        nc.vector.quantize_mx(
+            out=w_codes[:].bitcast(FP8X4), scales=w_scales[:], in_=w[:].rearrange("p q t -> p (q t)")
+        )
+        quantize_values(1)
+        inv_total = keep.tile([P, 1], F32, name="inv_total")
+        nc.vector.reciprocal(inv_total[:], total[:])
+
+        gate_tanh = keep.tile([P, DV], F32, name="gate_tanh")
+        gate = keep.tile([P, DV], F32, name="gate")
+        nc.scalar.activation(gate_tanh[:], gate_raw[:], ACT.Tanh, scale=0.5)
+        nc.vector.tensor_scalar(gate[:], gate_tanh[:], 1.0, inv_total[:], ADD, MULT)
+
+        result = keep.tile([P, DV], F32, name="result")
+        out_rows = out.rearrange("b q e -> (b q) e")
+        y = []
+        for b in range(2):
+            cols = slice(b * P, (b + 1) * P)
+            acc = psum.tile([P, P], F32, name="y%d" % b, tag="bank_%s" % "ab"[b])
+            nc.tensor.matmul_mx(
+                out=acc[:],
+                lhsT=w_codes[:].bitcast(FP8X4),
+                lhsT_scale=w_scales[:],
+                rhs=v_codes[:, cols].bitcast(FP8X4),
+                rhs_scale=v_scales[:, cols],
+                start=True,
+                stop=True,
+            )
+            y.append(acc)
+        for b in range(2):
+            cols = slice(b * P, (b + 1) * P)
+            nc.vector.scalar_tensor_tensor(result[:, cols], y[b][:], 0.5, gate[:, cols], MULT, MULT)
+            nc.sync.dma_start(out=out_rows[:, cols], in_=result[:, cols])

@@ -64,11 +64,6 @@ def tile_attend_x_norm_gate_topk_kernel(tc, qT, kT, vT, vs, kb, og, offs, out):
         nc.scalar.activation(warm_out[:], warm[:], ACT.Exp)
 
         k_grouped = keep.tile([P, N, PACK], BF16, name="k_grouped", align_bytes=64)
-        idle_bank = psum.tile([P, 4, P], F32, name="idle_bank", tag="bank_idle")
-
-        def keep_clock(pool, count):
-            for c in range(count):
-                nc.tensor.transpose(idle_bank[:, c % 4, :], pool[:, c * P : (c + 1) * P], ident[:])
 
         nc.vector.tensor_copy(k_grouped[:, :, 0], k_pool[0][:].indirect(offsets[:]))
         kb_row = keep.tile([P, N], F32, name="kb_row")
@@ -103,8 +98,6 @@ def tile_attend_x_norm_gate_topk_kernel(tc, qT, kT, vT, vs, kb, og, offs, out):
             out=q_codes[:].bitcast(FP8X4), scales=q_scales[:], in_=q_grouped[:].rearrange("p q t -> p (q t)")
         )
 
-        keep_clock(k_pool[2], 14)
-        keep_clock(k_pool[3], 14)
         k_codes = keep.tile([P, N], U32, name="k_codes", align_bytes=64)
         k_scales = keep.tile([P, N], U8, name="k_scales", align_bytes=64)
         k_flat = k_grouped[:].rearrange("p n t -> p (n t)")
@@ -161,11 +154,9 @@ def tile_attend_x_norm_gate_topk_kernel(tc, qT, kT, vT, vs, kb, og, offs, out):
                 out=v_codes[:, cols].bitcast(FP8X4), scales=v_scales[:, cols], in_=v_grouped[b][:]
             )
 
-        keep_clock(v_pool[0], 10)
         nc.vector.tensor_copy(v_cast[:, T // 2 :], v_pool[0][:, T // 2 :])
         nc.scalar.activation(v_cast[:, : T // 2], v_pool[0][:, : T // 2], ACT.Copy)
         gather_values(0)
-        keep_clock(v_pool[1], 8)
         for h in range(2):
             cols = slice(h * half, (h + 1) * half)
             nc.vector.tensor_tensor(neg_s[:, cols], neg_kb[:, cols], scores[h][:], SUB)

@@ -10,11 +10,9 @@ U16 = mybir.dt.uint16
 U8 = mybir.dt.uint8
 FP8X4 = mybir.dt.float8_e4m3fn_x4
 ADD = mybir.AluOpType.add
-SUB = mybir.AluOpType.subtract
 MULT = mybir.AluOpType.mult
 MIN = mybir.AluOpType.min
 ACT = mybir.ActivationFunctionType
-AXIS_X = mybir.AxisListType.X
 
 P = 128
 PACK = 4
@@ -23,6 +21,7 @@ T = 2048
 D = 512
 DV = 256
 NQ = 128
+CHUNK = 512
 
 FLOPS = 2 * NQ * N * D + 2 * NQ * N * DV
 BYTES = 4 * (D * NQ + D * T + DV * T + 2 * T + 2 * NQ * DV) + 2 * P * (N // 16)
@@ -37,7 +36,8 @@ def tile_attend_x_norm_gate_topk_kernel(tc, qT, kT, vT, vs, kb, og, offs, out):
         offsets = keep.tile([P, N // 16], U16, name="offsets")
         q_raw = keep.tile([P, PACK, NQ], F32, name="q_raw")
         k_pool = [keep.tile([P, T], F32, name="k_pool%d" % t) for t in range(PACK)]
-        v_pool = [keep.tile([P, T], F32, name="v_pool%d" % b) for b in range(2)]
+        v0_parts = [keep.tile([P, CHUNK], F32, name="v0_part%d" % c) for c in range(T // CHUNK)]
+        v1_pool = keep.tile([P, T], F32, name="v1_pool")
         kb_pool = keep.tile([P, T], F32, name="kb_pool")
         vs_pool = keep.tile([P, T], F32, name="vs_pool")
         gate_raw = keep.tile([P, DV], F32, name="gate_raw")
@@ -47,17 +47,18 @@ def tile_attend_x_norm_gate_topk_kernel(tc, qT, kT, vT, vs, kb, og, offs, out):
         nc.vector.memset(warm[:], 0.0)
         nc.vector.memset(kb_pool[:], 0.0)
         nc.vector.memset(vs_pool[:], 0.0)
-        nc.sync.dma_start(offsets[:], offs)
         k_rows = kT.rearrange("(p t) n -> p t n", t=PACK)
         for t in range(PACK):
             nc.sync.dma_start(out=k_pool[t][:], in_=k_rows[:, t, :])
             if t == 0:
+                nc.sync.dma_start(offsets[:], offs)
                 nc.sync.dma_start(out=kb_pool[0:1, :], in_=kb[0:1, :])
             if t == 1:
                 nc.sync.dma_start(out=vs_pool[0:1, :], in_=vs[0:1, :])
         nc.sync.dma_start(out=q_raw[:], in_=qT.rearrange("b (p t) q -> p (b t) q", t=PACK))
-        for b in range(2):
-            nc.sync.dma_start(out=v_pool[b][:], in_=vT[b * P : (b + 1) * P, :])
+        for c, part in enumerate(v0_parts):
+            nc.sync.dma_start(out=part[:], in_=vT[0:P, c * CHUNK : (c + 1) * CHUNK])
+        nc.sync.dma_start(out=v1_pool[:], in_=vT[P : 2 * P, :])
         nc.sync.dma_start(out=gate_raw[:], in_=og.rearrange("b q e -> (b q) e"))
         make_identity(nc, ident[:])
         warm_out = keep.tile([P, 1], F32, name="warm_out")
@@ -65,7 +66,8 @@ def tile_attend_x_norm_gate_topk_kernel(tc, qT, kT, vT, vs, kb, og, offs, out):
 
         k_grouped = keep.tile([P, N, PACK], BF16, name="k_grouped", align_bytes=64)
 
-        nc.vector.tensor_copy(k_grouped[:, :, 0], k_pool[0][:].indirect(offsets[:]))
+        k_low = keep.tile([P, 2, N], BF16, name="k_low")
+        nc.vector.tensor_copy(k_low[:, 0, :], k_pool[0][:].indirect(offsets[:]))
         kb_row = keep.tile([P, N], F32, name="kb_row")
         nc.vector.tensor_copy(kb_row[:], kb_pool[:].indirect(offsets[:]))
         kb_turned = psum.tile([P, 4, P], F32, name="kb_turned", tag="bank_a")
@@ -76,10 +78,11 @@ def tile_attend_x_norm_gate_topk_kernel(tc, qT, kT, vT, vs, kb, og, offs, out):
         kb_spread = psum.tile([P, 4, P], F32, name="kb_spread", tag="bank_b")
         for c in range(4):
             nc.tensor.transpose(kb_spread[:, c, :], kb_cols[:, c : c + 1].to_broadcast([P, P]), ident[:])
-        neg_kb = keep.tile([P, N], F32, name="neg_kb")
-        nc.scalar.activation(neg_kb[:], kb_spread[:].rearrange("p c q -> p (c q)"), ACT.Copy, scale=-1.0)
+        kb_all = keep.tile([P, N], F32, name="kb_all")
+        nc.scalar.copy(kb_all[:], kb_spread[:].rearrange("p c q -> p (c q)"))
 
-        nc.vector.tensor_copy(k_grouped[:, :, 1], k_pool[1][:].indirect(offsets[:]))
+        nc.vector.tensor_copy(k_low[:, 1, :], k_pool[1][:].indirect(offsets[:]))
+        nc.scalar.copy(k_grouped[:, :, 0:2], k_low[:].rearrange("p t n -> p n t"))
         vs_row = keep.tile([P, N], F32, name="vs_row")
         nc.vector.tensor_copy(vs_row[:], vs_pool[:].indirect(offsets[:]))
         vs_turned = psum.tile([P, PACK, P], F32, name="vs_turned", tag="bank_a")
@@ -89,7 +92,12 @@ def tile_attend_x_norm_gate_topk_kernel(tc, qT, kT, vT, vs, kb, og, offs, out):
         nc.scalar.copy(vs_cols[:], vs_turned[:, :, 0])
 
         nc.vector.tensor_copy(k_grouped[:, :, 2], k_pool[2][:].indirect(offsets[:]))
-        nc.vector.tensor_copy(k_grouped[:, :, 3], k_pool[3][:].indirect(offsets[:]))
+        half = N // 2
+        for h in range(2):
+            nc.vector.tensor_copy(
+                k_grouped[:, h * half : (h + 1) * half, 3],
+                k_pool[3][:].indirect(offsets[:, h * half // 16 : (h + 1) * half // 16]),
+            )
         q_grouped = keep.tile([P, NQ, PACK], BF16, name="q_grouped", align_bytes=64)
         q_codes = keep.tile([P, NQ], U32, name="q_codes", align_bytes=64)
         q_scales = keep.tile([P, NQ], U8, name="q_scales", align_bytes=64)
@@ -101,7 +109,6 @@ def tile_attend_x_norm_gate_topk_kernel(tc, qT, kT, vT, vs, kb, og, offs, out):
         k_codes = keep.tile([P, N], U32, name="k_codes", align_bytes=64)
         k_scales = keep.tile([P, N], U8, name="k_scales", align_bytes=64)
         k_flat = k_grouped[:].rearrange("p n t -> p (n t)")
-        half = N // 2
         for h in range(2):
             nc.vector.quantize_mx(
                 out=k_codes[:, h * half : (h + 1) * half].bitcast(FP8X4),
@@ -109,6 +116,7 @@ def tile_attend_x_norm_gate_topk_kernel(tc, qT, kT, vT, vs, kb, og, offs, out):
                 in_=k_flat[:, h * half * PACK : (h + 1) * half * PACK],
             )
         scores = [psum.tile([P, half], F32, name="scores%d" % h, tag="bank_s%d" % h) for h in range(2)]
+        s = keep.tile([P, N], F32, name="s")
         neg_s = keep.tile([P, N], F32, name="neg_s")
         for h in range(2):
             cols = slice(h * half, (h + 1) * half)
@@ -126,22 +134,21 @@ def tile_attend_x_norm_gate_topk_kernel(tc, qT, kT, vT, vs, kb, og, offs, out):
         v_codes = keep.tile([P, DV], U32, name="v_codes", align_bytes=64)
         v_scales = keep.tile([P, DV], U8, name="v_scales", align_bytes=64)
 
-        v_cast = keep.tile([P, T], BF16, name="v_cast")
+        v_cast = keep.tile([P, T], BF16, name="v_cast", tag="v_cast_then_p")
 
         def gather_values(b):
-            words = keep.tile([P, 2, P, 2], BF16, name="v_words%d" % b)
-            columns = words[:].rearrange("e u s r -> e s u r")
+            picked = keep.tile([P, N], BF16, name="v_picked%d" % b)
             if b == 0:
-                nc.scalar.activation(columns, v_cast[:].indirect(offsets[:]), ACT.Copy)
+                nc.scalar.activation(picked[:], v_cast[:].indirect(offsets[:]), ACT.Copy)
             else:
-                nc.vector.tensor_copy(columns, v_pool[b][:].indirect(offsets[:]))
-            v_words.append(words)
+                nc.vector.tensor_copy(picked[:], v1_pool[:].indirect(offsets[:]))
+            v_words.append(picked)
 
         def turn_values(b):
-            words = v_words[b][:].rearrange("e u s r -> e (u s r)").bitcast(F32)
+            words = v_words[b][:].bitcast(F32)
             turned = psum.tile([P, 2, P], F32, name="v_turned%d" % b, tag="bank_v%d" % b)
             for u in range(2):
-                nc.tensor.transpose(turned[:, u, :], words[:, u * P : (u + 1) * P], ident[:])
+                nc.tensor.transpose(turned[:, u, :], words[:, u : N // 2 : 2], ident[:])
             grouped = keep.tile([P, P * PACK], BF16, name="v_grouped%d" % b, align_bytes=64)
             nc.scalar.copy(
                 grouped[:].bitcast(F32).rearrange("s (e u) -> s e u", u=2), turned[:].rearrange("s u e -> s e u")
@@ -154,16 +161,16 @@ def tile_attend_x_norm_gate_topk_kernel(tc, qT, kT, vT, vs, kb, og, offs, out):
                 out=v_codes[:, cols].bitcast(FP8X4), scales=v_scales[:, cols], in_=v_grouped[b][:]
             )
 
-        nc.vector.tensor_copy(v_cast[:, T // 2 :], v_pool[0][:, T // 2 :])
-        nc.scalar.activation(v_cast[:, : T // 2], v_pool[0][:, : T // 2], ACT.Copy)
+        for c, part in enumerate(v0_parts):
+            nc.scalar.activation(v_cast[:, c * CHUNK : (c + 1) * CHUNK], part[:], ACT.Copy)
         gather_values(0)
         for h in range(2):
             cols = slice(h * half, (h + 1) * half)
-            nc.vector.tensor_tensor(neg_s[:, cols], neg_kb[:, cols], scores[h][:], SUB)
+            nc.vector.tensor_tensor(s[:, cols], kb_all[:, cols], scores[h][:], ADD)
         neg_m = keep.tile([P, 1], F32, name="neg_m")
-        nc.vector.tensor_reduce(neg_m[:], neg_s[:], AXIS_X, MIN)
+        nc.vector.tensor_scalar(neg_s[:], s[:], -1.0, None, MULT, MIN, accum_out=neg_m[:])
 
-        p = keep.tile([P, PACK, P], F32, name="p")
+        p = keep.tile([P, PACK, P], F32, name="p", tag="v_cast_then_p")
         total = keep.tile([P, 1], F32, name="total")
         nc.scalar.activation(
             p[:].rearrange("q t s -> q s t"),
@@ -173,10 +180,10 @@ def tile_attend_x_norm_gate_topk_kernel(tc, qT, kT, vT, vs, kb, og, offs, out):
             scale=-1.0,
             accum_out=total[:],
         )
+        turn_values(0)
         p_turned = psum.tile([P, PACK, NQ], F32, name="p_turned", tag="bank_p")
         for t in range(PACK):
             nc.tensor.transpose(p_turned[:, t, :], p[:, t, :], ident[:])
-        turn_values(0)
         gather_values(1)
         quantize_values(0)
         w = keep.tile([P, NQ, PACK], BF16, name="w", align_bytes=64)

@@ -36,8 +36,8 @@ def tile_attend_x_norm_gate_topk_kernel(tc, qT, kT, vT, vs, kb, og, offs, out):
         offsets = keep.tile([P, N // 16], U16, name="offsets")
         q_raw = keep.tile([P, PACK, NQ], F32, name="q_raw")
         k_pool = [keep.tile([P, T], F32, name="k_pool%d" % t) for t in range(PACK)]
-        v0_parts = [keep.tile([P, CHUNK], F32, name="v0_part%d" % c) for c in range(T // CHUNK)]
-        v1_pool = keep.tile([P, T], F32, name="v1_pool")
+        v0_pool = keep.tile([P, T], F32, name="v0_pool")
+        v1_pool = keep.tile([P, T], F32, name="v1_pool", tag="v1_pool_then_w", align_bytes=64)
         kb_pool = keep.tile([P, T], F32, name="kb_pool")
         vs_pool = keep.tile([P, T], F32, name="vs_pool")
         gate_raw = keep.tile([P, DV], F32, name="gate_raw")
@@ -56,8 +56,8 @@ def tile_attend_x_norm_gate_topk_kernel(tc, qT, kT, vT, vs, kb, og, offs, out):
             if t == 1:
                 nc.sync.dma_start(out=vs_pool[0:1, :], in_=vs[0:1, :])
         nc.sync.dma_start(out=q_raw[:], in_=qT.rearrange("b (p t) q -> p (b t) q", t=PACK))
-        for c, part in enumerate(v0_parts):
-            nc.sync.dma_start(out=part[:], in_=vT[0:P, c * CHUNK : (c + 1) * CHUNK])
+        for c in range(0, T, CHUNK):
+            nc.sync.dma_start(out=v0_pool[:, c : c + CHUNK], in_=vT[0:P, c : c + CHUNK])
         nc.sync.dma_start(out=v1_pool[:], in_=vT[P : 2 * P, :])
         nc.sync.dma_start(out=gate_raw[:], in_=og.rearrange("b q e -> (b q) e"))
         make_identity(nc, ident[:])
@@ -88,7 +88,7 @@ def tile_attend_x_norm_gate_topk_kernel(tc, qT, kT, vT, vs, kb, og, offs, out):
         vs_turned = psum.tile([P, PACK, P], F32, name="vs_turned", tag="bank_a")
         for t in range(PACK):
             nc.tensor.transpose(vs_turned[:, t, :], vs_row[:, t:N:PACK], ident[:])
-        vs_cols = keep.tile([P, PACK], F32, name="vs_cols")
+        vs_cols = keep.tile([P, PACK], F32, name="vs_cols", tag="vs_then_v0_codes", align_bytes=64)
         nc.scalar.copy(vs_cols[:], vs_turned[:, :, 0])
 
         nc.vector.tensor_copy(k_grouped[:, :, 2], k_pool[2][:].indirect(offsets[:]))
@@ -129,23 +129,16 @@ def tile_attend_x_norm_gate_topk_kernel(tc, qT, kT, vT, vs, kb, og, offs, out):
                 start=True,
                 stop=True,
             )
-        v_words = []
         v_grouped = []
-        v_codes = keep.tile([P, DV], U32, name="v_codes", align_bytes=64)
-        v_scales = keep.tile([P, DV], U8, name="v_scales", align_bytes=64)
+        v_codes = []
+        v_scales = []
 
         v_cast = keep.tile([P, T], BF16, name="v_cast", tag="v_cast_then_p")
 
-        def gather_values(b):
-            picked = keep.tile([P, N], BF16, name="v_picked%d" % b)
-            if b == 0:
-                nc.scalar.activation(picked[:], v_cast[:].indirect(offsets[:]), ACT.Copy)
-            else:
-                nc.vector.tensor_copy(picked[:], v1_pool[:].indirect(offsets[:]))
-            v_words.append(picked)
+        v_picked = [keep.tile([P, N], BF16, name="v_picked%d" % b, tag="v_picked%d" % b) for b in range(2)]
 
         def turn_values(b):
-            words = v_words[b][:].bitcast(F32)
+            words = v_picked[b][:].bitcast(F32)
             turned = psum.tile([P, 2, P], F32, name="v_turned%d" % b, tag="bank_v%d" % b)
             for u in range(2):
                 nc.tensor.transpose(turned[:, u, :], words[:, u : N // 2 : 2], ident[:])
@@ -156,19 +149,23 @@ def tile_attend_x_norm_gate_topk_kernel(tc, qT, kT, vT, vs, kb, og, offs, out):
             v_grouped.append(grouped)
 
         def quantize_values(b):
-            cols = slice(b * P, (b + 1) * P)
-            nc.vector.quantize_mx(
-                out=v_codes[:, cols].bitcast(FP8X4), scales=v_scales[:, cols], in_=v_grouped[b][:]
-            )
+            codes = keep.tile([P, P], U32, name="v_codes%d" % b, tag=("vs_then_v0_codes", "v1_codes")[b], align_bytes=64)
+            scales = keep.tile([P, P], U8, name="v_scales%d" % b, align_bytes=64)
+            nc.vector.quantize_mx(out=codes[:].bitcast(FP8X4), scales=scales[:], in_=v_grouped[b][:])
+            v_codes.append(codes)
+            v_scales.append(scales)
 
-        for c, part in enumerate(v0_parts):
-            nc.scalar.activation(v_cast[:, c * CHUNK : (c + 1) * CHUNK], part[:], ACT.Copy)
-        gather_values(0)
+        for c in range(0, T, CHUNK):
+            nc.scalar.activation(v_cast[:, c : c + CHUNK], v0_pool[:, c : c + CHUNK], ACT.Copy)
+        nc.scalar.activation(v_picked[0][:, :half], v_cast[:].indirect(offsets[:, : half // 16]), ACT.Copy)
         for h in range(2):
             cols = slice(h * half, (h + 1) * half)
             nc.vector.tensor_tensor(s[:, cols], kb_all[:, cols], scores[h][:], ADD)
         neg_m = keep.tile([P, 1], F32, name="neg_m")
         nc.vector.tensor_scalar(neg_s[:], s[:], -1.0, None, MULT, MIN, accum_out=neg_m[:])
+
+        nc.vector.tensor_copy(v_picked[0][:, half:], v0_pool[:].indirect(offsets[:, half // 16 :]))
+        nc.vector.tensor_copy(v_picked[1][:], v1_pool[:].indirect(offsets[:]))
 
         p = keep.tile([P, PACK, P], F32, name="p", tag="v_cast_then_p")
         total = keep.tile([P, 1], F32, name="total")
@@ -184,9 +181,7 @@ def tile_attend_x_norm_gate_topk_kernel(tc, qT, kT, vT, vs, kb, og, offs, out):
         p_turned = psum.tile([P, PACK, NQ], F32, name="p_turned", tag="bank_p")
         for t in range(PACK):
             nc.tensor.transpose(p_turned[:, t, :], p[:, t, :], ident[:])
-        gather_values(1)
-        quantize_values(0)
-        w = keep.tile([P, NQ, PACK], BF16, name="w", align_bytes=64)
+        w = keep.tile([P, NQ, PACK], BF16, name="w", tag="v1_pool_then_w", align_bytes=64)
         w_codes = keep.tile([P, NQ], U32, name="w_codes", align_bytes=64)
         w_scales = keep.tile([P, NQ], U8, name="w_scales", align_bytes=64)
         nc.vector.tensor_tensor(
@@ -199,8 +194,9 @@ def tile_attend_x_norm_gate_topk_kernel(tc, qT, kT, vT, vs, kb, og, offs, out):
         nc.vector.quantize_mx(
             out=w_codes[:].bitcast(FP8X4), scales=w_scales[:], in_=w[:].rearrange("p q t -> p (q t)")
         )
+        quantize_values(0)
         quantize_values(1)
-        inv_total = keep.tile([P, 1], F32, name="inv_total")
+        inv_total = keep.tile([P, 1], F32, name="inv_total", tag="v_picked1")
         nc.vector.reciprocal(inv_total[:], total[:])
 
         gate_tanh = keep.tile([P, DV], F32, name="gate_tanh")
@@ -212,14 +208,13 @@ def tile_attend_x_norm_gate_topk_kernel(tc, qT, kT, vT, vs, kb, og, offs, out):
         out_rows = out.rearrange("b q e -> (b q) e")
         y = []
         for b in range(2):
-            cols = slice(b * P, (b + 1) * P)
             acc = psum.tile([P, P], F32, name="y%d" % b, tag="bank_%s" % "ab"[b])
             nc.tensor.matmul_mx(
                 out=acc[:],
                 lhsT=w_codes[:].bitcast(FP8X4),
                 lhsT_scale=w_scales[:],
-                rhs=v_codes[:, cols].bitcast(FP8X4),
-                rhs_scale=v_scales[:, cols],
+                rhs=v_codes[b][:].bitcast(FP8X4),
+                rhs_scale=v_scales[b][:],
                 start=True,
                 stop=True,
             )

@@ -157,26 +157,28 @@ def tile_attend_x_norm_gate_topk_kernel(tc, qT, kT, vT, vs, kb, og, offs, out):
 
         for c in range(0, T, CHUNK):
             nc.scalar.activation(v_cast[:, c : c + CHUNK], v0_pool[:, c : c + CHUNK], ACT.Copy)
-        nc.scalar.activation(v_picked[0][:, :half], v_cast[:].indirect(offsets[:, : half // 16]), ACT.Copy)
+        nc.scalar.activation(v_picked[0][:], v_cast[:].indirect(offsets[:]), ACT.Copy)
         for h in range(2):
             cols = slice(h * half, (h + 1) * half)
             nc.vector.tensor_tensor(s[:, cols], kb_all[:, cols], scores[h][:], ADD)
         neg_m = keep.tile([P, 1], F32, name="neg_m")
         nc.vector.tensor_scalar(neg_s[:], s[:], -1.0, None, MULT, MIN, accum_out=neg_m[:])
 
-        nc.vector.tensor_copy(v_picked[0][:, half:], v0_pool[:].indirect(offsets[:, half // 16 :]))
         nc.vector.tensor_copy(v_picked[1][:], v1_pool[:].indirect(offsets[:]))
 
         p = keep.tile([P, PACK, P], F32, name="p", tag="v_cast_then_p")
+        part = [keep.tile([P, 1], F32, name="part%d" % u) for u in range(2)]
+        for u in range(2):
+            nc.scalar.activation(
+                p[:, 2 * u : 2 * u + 2, :].rearrange("q r s -> q s r"),
+                neg_s[:].rearrange("q (s t) -> q s t", t=PACK)[:, :, 2 * u : 2 * u + 2],
+                ACT.Exp,
+                bias=neg_m[:],
+                scale=-1.0,
+                accum_out=part[u][:],
+            )
         total = keep.tile([P, 1], F32, name="total")
-        nc.scalar.activation(
-            p[:].rearrange("q t s -> q s t"),
-            neg_s[:].rearrange("q (s t) -> q s t", t=PACK),
-            ACT.Exp,
-            bias=neg_m[:],
-            scale=-1.0,
-            accum_out=total[:],
-        )
+        nc.scalar.activation(total[:], part[0][:], ACT.Identity, bias=part[1][:])
         turn_values(0)
         p_turned = psum.tile([P, PACK, NQ], F32, name="p_turned", tag="bank_p")
         for t in range(PACK):
@@ -202,7 +204,7 @@ def tile_attend_x_norm_gate_topk_kernel(tc, qT, kT, vT, vs, kb, og, offs, out):
         gate_tanh = keep.tile([P, DV], F32, name="gate_tanh")
         gate = keep.tile([P, DV], F32, name="gate")
         nc.scalar.activation(gate_tanh[:], gate_raw[:], ACT.Tanh, scale=0.5)
-        nc.vector.tensor_scalar(gate[:], gate_tanh[:], 1.0, inv_total[:], ADD, MULT)
+        nc.scalar.activation(gate[:], gate_tanh[:], ACT.Identity, bias=inv_total[:], scale=inv_total[:])
 
         result = keep.tile([P, DV], F32, name="result")
         out_rows = out.rearrange("b q e -> (b q) e")

@@ -22,6 +22,7 @@ D = 512
 DV = 256
 NQ = 128
 CHUNK = 512
+VS_ROW = 64
 
 FLOPS = 2 * NQ * N * D + 2 * NQ * N * DV
 BYTES = 4 * (D * NQ + D * T + DV * T + 2 * T + 2 * NQ * DV) + 2 * P * (N // 16)
@@ -54,7 +55,7 @@ def tile_attend_x_norm_gate_topk_kernel(tc, qT, kT, vT, vs, kb, og, offs, out):
                 nc.sync.dma_start(offsets[:], offs)
                 nc.sync.dma_start(out=kb_pool[0:1, :], in_=kb[0:1, :])
             if t == 1:
-                nc.sync.dma_start(out=vs_pool[0:1, :], in_=vs[0:1, :])
+                nc.sync.dma_start(out=vs_pool[VS_ROW : VS_ROW + 1, :], in_=vs[0:1, :])
         nc.sync.dma_start(out=q_raw[:], in_=qT.rearrange("b (p t) q -> p (b t) q", t=PACK))
         for c in range(0, T, CHUNK):
             nc.sync.dma_start(out=v0_pool[:, c : c + CHUNK], in_=vT[0:P, c : c + CHUNK])
@@ -89,7 +90,7 @@ def tile_attend_x_norm_gate_topk_kernel(tc, qT, kT, vT, vs, kb, og, offs, out):
         for t in range(PACK):
             nc.tensor.transpose(vs_turned[:, t, :], vs_row[:, t:N:PACK], ident[:])
         vs_cols = keep.tile([P, PACK], F32, name="vs_cols", tag="vs_then_v0_codes", align_bytes=64)
-        nc.scalar.copy(vs_cols[:], vs_turned[:, :, 0])
+        nc.scalar.copy(vs_cols[:], vs_turned[:, :, VS_ROW])
 
         nc.vector.tensor_copy(k_grouped[:, :, 2], k_pool[2][:].indirect(offsets[:]))
         half = N // 2

@@ -22,6 +22,7 @@ D = 512
 DV = 256
 NQ = 128
 CHUNK = 512
+SPLIT = 384
 VS_ROW = 64
 
 FLOPS = 2 * NQ * N * D + 2 * NQ * N * DV
@@ -32,13 +33,14 @@ def tile_attend_x_norm_gate_topk_kernel(tc, qT, kT, vT, vs, kb, og, offs, out):
     nc = tc.nc
     with ExitStack() as ctx:
         keep = ctx.enter_context(tc.tile_pool(name="keep", bufs=1))
+        late = ctx.enter_context(tc.tile_pool(name="late", bufs=1))
         psum = ctx.enter_context(tc.psum_pool(name="psum", bufs=1))
 
         offsets = keep.tile([P, N // 16], U16, name="offsets")
         q_raw = keep.tile([P, PACK, NQ], F32, name="q_raw")
         k_pool = [keep.tile([P, T], F32, name="k_pool%d" % t) for t in range(PACK)]
         v0_pool = keep.tile([P, T], F32, name="v0_pool")
-        v1_pool = keep.tile([P, T], F32, name="v1_pool", tag="v1_pool_then_w", align_bytes=64)
+        v1_pool = late.tile([P, T], F32, name="v1_pool", offset=0, align_bytes=64)
         kb_pool = keep.tile([P, T], F32, name="kb_pool")
         vs_pool = keep.tile([P, T], F32, name="vs_pool")
         gate_raw = keep.tile([P, DV], F32, name="gate_raw")
@@ -89,7 +91,7 @@ def tile_attend_x_norm_gate_topk_kernel(tc, qT, kT, vT, vs, kb, og, offs, out):
         vs_turned = psum.tile([P, PACK, P], F32, name="vs_turned", tag="bank_a")
         for t in range(PACK):
             nc.tensor.transpose(vs_turned[:, t, :], vs_row[:, t:N:PACK], ident[:])
-        vs_cols = keep.tile([P, PACK], F32, name="vs_cols", tag="vs_then_v0_codes", align_bytes=64)
+        vs_cols = keep.tile([P, PACK], F32, name="vs_cols")
         nc.scalar.copy(vs_cols[:], vs_turned[:, :, VS_ROW])
 
         nc.vector.tensor_copy(k_grouped[:, :, 2], k_pool[2][:].indirect(offsets[:]))
@@ -136,7 +138,7 @@ def tile_attend_x_norm_gate_topk_kernel(tc, qT, kT, vT, vs, kb, og, offs, out):
 
         v_cast = keep.tile([P, T], BF16, name="v_cast", tag="v_cast_then_p")
 
-        v_picked = [keep.tile([P, N], BF16, name="v_picked%d" % b, tag="v_picked%d" % b) for b in range(2)]
+        v_picked = [keep.tile([P, N], BF16, name="v_picked%d" % b) for b in range(2)]
 
         def turn_values(b):
             words = v_picked[b][:].bitcast(F32)
@@ -150,7 +152,7 @@ def tile_attend_x_norm_gate_topk_kernel(tc, qT, kT, vT, vs, kb, og, offs, out):
             v_grouped.append(grouped)
 
         def quantize_values(b):
-            codes = keep.tile([P, P], U32, name="v_codes%d" % b, tag=("vs_then_v0_codes", "v1_codes")[b], align_bytes=64)
+            codes = late.tile([P, P], U32, name="v_codes%d" % b, offset=2048 + 512 * b, align_bytes=64)
             scales = keep.tile([P, P], U8, name="v_scales%d" % b, align_bytes=64)
             nc.vector.quantize_mx(out=codes[:].bitcast(FP8X4), scales=scales[:], in_=v_grouped[b][:])
             v_codes.append(codes)
@@ -158,13 +160,14 @@ def tile_attend_x_norm_gate_topk_kernel(tc, qT, kT, vT, vs, kb, og, offs, out):
 
         for c in range(0, T, CHUNK):
             nc.scalar.activation(v_cast[:, c : c + CHUNK], v0_pool[:, c : c + CHUNK], ACT.Copy)
-        nc.scalar.activation(v_picked[0][:], v_cast[:].indirect(offsets[:]), ACT.Copy)
+        nc.scalar.activation(v_picked[0][:, :SPLIT], v_cast[:].indirect(offsets[:, : SPLIT // 16]), ACT.Copy)
         for h in range(2):
             cols = slice(h * half, (h + 1) * half)
             nc.vector.tensor_tensor(s[:, cols], kb_all[:, cols], scores[h][:], ADD)
         neg_m = keep.tile([P, 1], F32, name="neg_m")
         nc.vector.tensor_scalar(neg_s[:], s[:], -1.0, None, MULT, MIN, accum_out=neg_m[:])
 
+        nc.vector.tensor_copy(v_picked[0][:, SPLIT:], v0_pool[:].indirect(offsets[:, SPLIT // 16 :]))
         nc.vector.tensor_copy(v_picked[1][:], v1_pool[:].indirect(offsets[:]))
 
         p = keep.tile([P, PACK, P], F32, name="p", tag="v_cast_then_p")
@@ -184,7 +187,7 @@ def tile_attend_x_norm_gate_topk_kernel(tc, qT, kT, vT, vs, kb, og, offs, out):
         p_turned = psum.tile([P, PACK, NQ], F32, name="p_turned", tag="bank_p")
         for t in range(PACK):
             nc.tensor.transpose(p_turned[:, t, :], p[:, t, :], ident[:])
-        w = keep.tile([P, NQ, PACK], BF16, name="w", tag="v1_pool_then_w", align_bytes=64)
+        w = late.tile([P, NQ, PACK], BF16, name="w", offset=0, align_bytes=64)
         w_codes = keep.tile([P, NQ], U32, name="w_codes", align_bytes=64)
         w_scales = keep.tile([P, NQ], U8, name="w_scales", align_bytes=64)
         nc.vector.tensor_tensor(
@@ -194,18 +197,18 @@ def tile_attend_x_norm_gate_topk_kernel(tc, qT, kT, vT, vs, kb, og, offs, out):
             MULT,
         )
         turn_values(1)
+        quantize_values(0)
+        inv_total = late.tile([P, 1], F32, name="inv_total", offset=4096)
+        nc.vector.reciprocal(inv_total[:], total[:])
         nc.vector.quantize_mx(
             out=w_codes[:].bitcast(FP8X4), scales=w_scales[:], in_=w[:].rearrange("p q t -> p (q t)")
         )
-        quantize_values(0)
         quantize_values(1)
-        inv_total = keep.tile([P, 1], F32, name="inv_total", tag="v_picked1")
-        nc.vector.reciprocal(inv_total[:], total[:])
 
         gate_tanh = keep.tile([P, DV], F32, name="gate_tanh")
         gate = keep.tile([P, DV], F32, name="gate")
         nc.scalar.activation(gate_tanh[:], gate_raw[:], ACT.Tanh, scale=0.5)
-        nc.scalar.activation(gate[:], gate_tanh[:], ACT.Identity, bias=inv_total[:], scale=inv_total[:])
+        nc.scalar.activation(gate[:], gate_tanh[:], ACT.Copy, bias=0.5, scale=0.5)
 
         result = keep.tile([P, DV], F32, name="result")
         out_rows = out.rearrange("b q e -> (b q) e")
@@ -224,5 +227,5 @@ def tile_attend_x_norm_gate_topk_kernel(tc, qT, kT, vT, vs, kb, og, offs, out):
             y.append(acc)
         for b in range(2):
             cols = slice(b * P, (b + 1) * P)
-            nc.vector.scalar_tensor_tensor(result[:, cols], y[b][:], 0.5, gate[:, cols], MULT, MULT)
+            nc.vector.scalar_tensor_tensor(result[:, cols], y[b][:], inv_total[:], gate[:, cols], MULT, MULT)
             nc.sync.dma_start(out=out_rows[:, cols], in_=result[:, cols])

@@ -112,17 +112,18 @@ def tile_attend_x_norm_gate_topk_kernel(tc, qT, kT, vT, vs, kb, og, offs, out):
         k_codes = keep.tile([P, N], U32, name="k_codes", align_bytes=64)
         k_scales = keep.tile([P, N], U8, name="k_scales", align_bytes=64)
         k_flat = k_grouped[:].rearrange("p n t -> p (n t)")
-        for h in range(2):
+        for h in range(N // P):
             nc.vector.quantize_mx(
-                out=k_codes[:, h * half : (h + 1) * half].bitcast(FP8X4),
-                scales=k_scales[:, h * half : (h + 1) * half],
-                in_=k_flat[:, h * half * PACK : (h + 1) * half * PACK],
+                out=k_codes[:, h * P : (h + 1) * P].bitcast(FP8X4),
+                scales=k_scales[:, h * P : (h + 1) * P],
+                in_=k_flat[:, h * P * PACK : (h + 1) * P * PACK],
             )
-        scores = [psum.tile([P, half], F32, name="scores%d" % h, tag="bank_s%d" % h) for h in range(2)]
+        score_banks = ["bank_s0", "bank_s1", "bank_s2", "bank_p"]
+        scores = [psum.tile([P, P], F32, name="scores%d" % h, tag=score_banks[h]) for h in range(N // P)]
         s = keep.tile([P, N], F32, name="s")
         neg_s = keep.tile([P, N], F32, name="neg_s")
-        for h in range(2):
-            cols = slice(h * half, (h + 1) * half)
+        for h in range(N // P):
+            cols = slice(h * P, (h + 1) * P)
             nc.tensor.matmul_mx(
                 out=scores[h][:],
                 lhsT=q_codes[:].bitcast(FP8X4),
@@ -161,8 +162,8 @@ def tile_attend_x_norm_gate_topk_kernel(tc, qT, kT, vT, vs, kb, og, offs, out):
         for c in range(0, T, CHUNK):
             nc.scalar.activation(v_cast[:, c : c + CHUNK], v0_pool[:, c : c + CHUNK], ACT.Copy)
         nc.scalar.activation(v_picked[0][:, :SPLIT], v_cast[:].indirect(offsets[:, : SPLIT // 16]), ACT.Copy)
-        for h in range(2):
-            cols = slice(h * half, (h + 1) * half)
+        for h in range(N // P):
+            cols = slice(h * P, (h + 1) * P)
             nc.vector.tensor_tensor(s[:, cols], kb_all[:, cols], scores[h][:], ADD)
         neg_m = keep.tile([P, 1], F32, name="neg_m")
         nc.vector.tensor_scalar(neg_s[:], s[:], -1.0, None, MULT, MIN, accum_out=neg_m[:])

@@ -75,7 +75,7 @@ def tile_attend_x_norm_gate_topk_kernel(tc, qT, kT, vT, vs, kb, og, offs, out):
         nc.vector.tensor_copy(kb_row[:], kb_pool[:].indirect(offsets[:]))
         kb_turned = psum.tile([P, 4, P], F32, name="kb_turned", tag="bank_a")
         for c in range(4):
-            nc.tensor.transpose(kb_turned[:, c, :], kb_row[:, c * P : (c + 1) * P], ident[:])
+            nc.tensor.transpose(kb_turned[:, c, :], kb_row[:, c:N:PACK], ident[:])
         kb_cols = keep.tile([P, 4], F32, name="kb_cols")
         nc.scalar.copy(kb_cols[:], kb_turned[:, :, 0])
         kb_spread = psum.tile([P, 4, P], F32, name="kb_spread", tag="bank_b")
@@ -163,8 +163,13 @@ def tile_attend_x_norm_gate_topk_kernel(tc, qT, kT, vT, vs, kb, og, offs, out):
             nc.scalar.activation(v_cast[:, c : c + CHUNK], v0_pool[:, c : c + CHUNK], ACT.Copy)
         nc.scalar.activation(v_picked[0][:, :SPLIT], v_cast[:].indirect(offsets[:, : SPLIT // 16]), ACT.Copy)
         for h in range(N // P):
-            cols = slice(h * P, (h + 1) * P)
-            nc.vector.tensor_tensor(s[:, cols], kb_all[:, cols], scores[h][:], ADD)
+            run = slice(h * P // PACK, (h + 1) * P // PACK)
+            nc.vector.tensor_tensor(
+                s[:].rearrange("q (t s) -> q t s", t=PACK)[:, :, run],
+                kb_all[:].rearrange("q (t s) -> q t s", t=PACK)[:, :, run],
+                scores[h][:].rearrange("q (s t) -> q t s", t=PACK),
+                ADD,
+            )
         neg_m = keep.tile([P, 1], F32, name="neg_m")
         nc.vector.tensor_scalar(neg_s[:], s[:], -1.0, None, MULT, MIN, accum_out=neg_m[:])
 
@@ -175,8 +180,8 @@ def tile_attend_x_norm_gate_topk_kernel(tc, qT, kT, vT, vs, kb, og, offs, out):
         part = [keep.tile([P, 1], F32, name="part%d" % u) for u in range(2)]
         for u in range(2):
             nc.scalar.activation(
-                p[:, 2 * u : 2 * u + 2, :].rearrange("q r s -> q s r"),
-                neg_s[:].rearrange("q (s t) -> q s t", t=PACK)[:, :, 2 * u : 2 * u + 2],
+                p[:, 2 * u : 2 * u + 2, :].rearrange("q r s -> q (r s)"),
+                neg_s[:, 2 * u * P : (2 * u + 2) * P],
                 ACT.Exp,
                 bias=neg_m[:],
                 scale=-1.0,

@@ -44,10 +44,8 @@ def tile_attend_x_norm_gate_topk_kernel(tc, qT, kT, vT, vs, kb, og, offs, out):
         kb_pool = keep.tile([P, T], F32, name="kb_pool")
         vs_pool = keep.tile([P, T], F32, name="vs_pool")
         gate_raw = keep.tile([P, DV], F32, name="gate_raw")
-        warm = keep.tile([P, 1], F32, name="warm")
         ident = keep.tile([P, P], F32, name="ident")
 
-        nc.vector.memset(warm[:], 0.0)
         nc.vector.memset(kb_pool[:], 0.0)
         nc.vector.memset(vs_pool[:], 0.0)
         k_rows = kT.rearrange("(p t) n -> p t n", t=PACK)
@@ -64,8 +62,6 @@ def tile_attend_x_norm_gate_topk_kernel(tc, qT, kT, vT, vs, kb, og, offs, out):
         nc.sync.dma_start(out=v1_pool[:], in_=vT[P : 2 * P, :])
         nc.sync.dma_start(out=gate_raw[:], in_=og.rearrange("b q e -> (b q) e"))
         make_identity(nc, ident[:])
-        warm_out = keep.tile([P, 1], F32, name="warm_out")
-        nc.scalar.activation(warm_out[:], warm[:], ACT.Exp)
 
         k_grouped = keep.tile([P, N, PACK], BF16, name="k_grouped", align_bytes=64)
 

@@ -11,7 +11,7 @@ U8 = mybir.dt.uint8
 FP8X4 = mybir.dt.float8_e4m3fn_x4
 ADD = mybir.AluOpType.add
 MULT = mybir.AluOpType.mult
-MIN = mybir.AluOpType.min
+MAX = mybir.AluOpType.max
 ACT = mybir.ActivationFunctionType
 
 P = 128
@@ -21,8 +21,8 @@ T = 2048
 D = 512
 DV = 256
 NQ = 128
-CHUNK = 512
-SPLIT = 384
+CHUNKS = (0, 640, 1216, 1664, 2048)
+SPLIT = 416
 VS_ROW = 64
 
 FLOPS = 2 * NQ * N * D + 2 * NQ * N * DV
@@ -57,8 +57,8 @@ def tile_attend_x_norm_gate_topk_kernel(tc, qT, kT, vT, vs, kb, og, offs, out):
             if t == 1:
                 nc.sync.dma_start(out=vs_pool[VS_ROW : VS_ROW + 1, :], in_=vs[0:1, :])
         nc.sync.dma_start(out=q_raw[:], in_=qT.rearrange("b (p t) q -> p (b t) q", t=PACK))
-        for c in range(0, T, CHUNK):
-            nc.sync.dma_start(out=v0_pool[:, c : c + CHUNK], in_=vT[0:P, c : c + CHUNK])
+        for a, b in zip(CHUNKS, CHUNKS[1:]):
+            nc.sync.dma_start(out=v0_pool[:, a:b], in_=vT[0:P, a:b])
         nc.sync.dma_start(out=v1_pool[:], in_=vT[P : 2 * P, :])
         nc.sync.dma_start(out=gate_raw[:], in_=og.rearrange("b q e -> (b q) e"))
         make_identity(nc, ident[:])
@@ -117,7 +117,6 @@ def tile_attend_x_norm_gate_topk_kernel(tc, qT, kT, vT, vs, kb, og, offs, out):
         score_banks = ["bank_s0", "bank_s1", "bank_s2", "bank_p"]
         scores = [psum.tile([P, P], F32, name="scores%d" % h, tag=score_banks[h]) for h in range(N // P)]
         s = keep.tile([P, N], F32, name="s")
-        neg_s = keep.tile([P, N], F32, name="neg_s")
         for h in range(N // P):
             cols = slice(h * P, (h + 1) * P)
             nc.tensor.matmul_mx(
@@ -155,8 +154,8 @@ def tile_attend_x_norm_gate_topk_kernel(tc, qT, kT, vT, vs, kb, og, offs, out):
             v_codes.append(codes)
             v_scales.append(scales)
 
-        for c in range(0, T, CHUNK):
-            nc.scalar.activation(v_cast[:, c : c + CHUNK], v0_pool[:, c : c + CHUNK], ACT.Copy)
+        for a, b in zip(CHUNKS, CHUNKS[1:]):
+            nc.scalar.activation(v_cast[:, a:b], v0_pool[:, a:b], ACT.Copy)
         nc.scalar.activation(v_picked[0][:, :SPLIT], v_cast[:].indirect(offsets[:, : SPLIT // 16]), ACT.Copy)
         for h in range(N // P):
             run = slice(h * P // PACK, (h + 1) * P // PACK)
@@ -167,7 +166,7 @@ def tile_attend_x_norm_gate_topk_kernel(tc, qT, kT, vT, vs, kb, og, offs, out):
                 ADD,
             )
         neg_m = keep.tile([P, 1], F32, name="neg_m")
-        nc.vector.tensor_scalar(neg_s[:], s[:], -1.0, None, MULT, MIN, accum_out=neg_m[:])
+        nc.vector.tensor_reduce(neg_m[:], s[:], mybir.AxisListType.X, MAX, negate=True)
 
         nc.vector.tensor_copy(v_picked[0][:, SPLIT:], v0_pool[:].indirect(offsets[:, SPLIT // 16 :]))
         nc.vector.tensor_copy(v_picked[1][:], v1_pool[:].indirect(offsets[:]))
@@ -177,10 +176,9 @@ def tile_attend_x_norm_gate_topk_kernel(tc, qT, kT, vT, vs, kb, og, offs, out):
         for u in range(2):
             nc.scalar.activation(
                 p[:, 2 * u : 2 * u + 2, :].rearrange("q r s -> q (r s)"),
-                neg_s[:, 2 * u * P : (2 * u + 2) * P],
+                s[:, 2 * u * P : (2 * u + 2) * P],
                 ACT.Exp,
                 bias=neg_m[:],
-                scale=-1.0,
                 accum_out=part[u][:],
             )
         total = keep.tile([P, 1], F32, name="total")

@@ -140,7 +140,8 @@ def tile_attend_x_norm_gate_topk_kernel(tc, qT, kT, vT, vs, kb, og, offs, out):
             words = v_picked[b][:].bitcast(F32)
             turned = psum.tile([P, 2, P], F32, name="v_turned%d" % b, tag="bank_v%d" % b)
             for u in range(2):
-                nc.tensor.transpose(turned[:, u, :], words[:, u : N // 2 : 2], ident[:])
+                picked = words[:, u : N // 2 : 2] if b == 0 else words[:, u * P : (u + 1) * P]
+                nc.tensor.transpose(turned[:, u, :], picked, ident[:])
             grouped = keep.tile([P, P * PACK], BF16, name="v_grouped%d" % b, align_bytes=64)
             nc.scalar.copy(
                 grouped[:].bitcast(F32).rearrange("s (e u) -> s e u", u=2), turned[:].rearrange("s u e -> s e u")
@@ -169,7 +170,9 @@ def tile_attend_x_norm_gate_topk_kernel(tc, qT, kT, vT, vs, kb, og, offs, out):
         nc.vector.tensor_reduce(neg_m[:], s[:], mybir.AxisListType.X, MAX, negate=True)
 
         nc.vector.tensor_copy(v_picked[0][:, SPLIT:], v0_pool[:].indirect(offsets[:, SPLIT // 16 :]))
-        nc.vector.tensor_copy(v_picked[1][:], v1_pool[:].indirect(offsets[:]))
+        nc.vector.tensor_copy(
+            v_picked[1][:].rearrange("e (u s j) -> e s u j", u=2, j=2), v1_pool[:].indirect(offsets[:])
+        )
 
         p = keep.tile([P, PACK, P], F32, name="p", tag="v_cast_then_p")
         part = [keep.tile([P, 1], F32, name="part%d" % u) for u in range(2)]

@@ -193,19 +193,24 @@ def tile_attend_x_norm_gate_topk_kernel(tc, qT, kT, vT, vs, kb, og, offs, out):
         w = late.tile([P, NQ, PACK], BF16, name="w", offset=0, align_bytes=64)
         w_codes = keep.tile([P, NQ], U32, name="w_codes", align_bytes=64)
         w_scales = keep.tile([P, NQ], U8, name="w_scales", align_bytes=64)
-        nc.vector.tensor_tensor(
-            w[:],
-            p_turned[:].rearrange("s t q -> s q t"),
-            vs_cols[:].unsqueeze(1).to_broadcast([P, NQ, PACK]),
-            MULT,
-        )
+        q_halves = [slice(0, NQ // 2), slice(NQ // 2, NQ)]
+        for rows in q_halves:
+            nc.vector.tensor_tensor(
+                w[:, rows, :],
+                p_turned[:].rearrange("s t q -> s q t")[:, rows, :],
+                vs_cols[:].unsqueeze(1).to_broadcast([P, NQ // 2, PACK]),
+                MULT,
+            )
         turn_values(1)
         quantize_values(0)
         inv_total = late.tile([P, 1], F32, name="inv_total", offset=4096)
         nc.vector.reciprocal(inv_total[:], total[:])
-        nc.vector.quantize_mx(
-            out=w_codes[:].bitcast(FP8X4), scales=w_scales[:], in_=w[:].rearrange("p q t -> p (q t)")
-        )
+        for rows in q_halves:
+            nc.vector.quantize_mx(
+                out=w_codes[:, rows].bitcast(FP8X4),
+                scales=w_scales[:, rows],
+                in_=w[:, rows, :].rearrange("p q t -> p (q t)"),
+            )
         quantize_values(1)
 
         gate_tanh = keep.tile([P, DV], F32, name="gate_tanh")

@@ -22,7 +22,7 @@ D = 512
 DV = 256
 NQ = 128
 CHUNKS = (0, 640, 1216, 1664, 2048)
-SPLIT = 416
+SPLIT = 352
 VS_ROW = 64
 
 FLOPS = 2 * NQ * N * D + 2 * NQ * N * DV
@@ -37,7 +37,7 @@ def tile_attend_x_norm_gate_topk_kernel(tc, qT, kT, vT, vs, kb, og, offs, out):
         psum = ctx.enter_context(tc.psum_pool(name="psum", bufs=1))
 
         offsets = keep.tile([P, N // 16], U16, name="offsets")
-        q_raw = keep.tile([P, PACK, NQ], F32, name="q_raw")
+        q_raw = late.tile([P, PACK, NQ], F32, name="q_raw", offset=8192 + 512, align_bytes=64)
         k_pool = [keep.tile([P, T], F32, name="k_pool%d" % t) for t in range(PACK)]
         v0_pool = keep.tile([P, T], F32, name="v0_pool")
         v1_pool = late.tile([P, T], F32, name="v1_pool", offset=0, align_bytes=64)
@@ -105,12 +105,14 @@ def tile_attend_x_norm_gate_topk_kernel(tc, qT, kT, vT, vs, kb, og, offs, out):
             out=q_codes[:].bitcast(FP8X4), scales=q_scales[:], in_=q_grouped[:].rearrange("p q t -> p (q t)")
         )
 
-        k_codes = keep.tile([P, N], U32, name="k_codes", align_bytes=64)
+        k_codes = [
+            late.tile([P, P], U32, name="k_codes%d" % h, offset=8192 + 512 * h, align_bytes=64) for h in range(N // P)
+        ]
         k_scales = keep.tile([P, N], U8, name="k_scales", align_bytes=64)
         k_flat = k_grouped[:].rearrange("p n t -> p (n t)")
         for h in range(N // P):
             nc.vector.quantize_mx(
-                out=k_codes[:, h * P : (h + 1) * P].bitcast(FP8X4),
+                out=k_codes[h][:].bitcast(FP8X4),
                 scales=k_scales[:, h * P : (h + 1) * P],
                 in_=k_flat[:, h * P * PACK : (h + 1) * P * PACK],
             )
@@ -123,7 +125,7 @@ def tile_attend_x_norm_gate_topk_kernel(tc, qT, kT, vT, vs, kb, og, offs, out):
                 out=scores[h][:],
                 lhsT=q_codes[:].bitcast(FP8X4),
                 lhsT_scale=q_scales[:],
-                rhs=k_codes[:, cols].bitcast(FP8X4),
+                rhs=k_codes[h][:].bitcast(FP8X4),
                 rhs_scale=k_scales[:, cols],
                 start=True,
                 stop=True,

@@ -22,7 +22,7 @@ D = 512
 DV = 256
 NQ = 128
 CHUNKS = (0, 640, 1216, 1664, 2048)
-SPLIT = 352
+SPLIT = 384
 VS_ROW = 64
 
 FLOPS = 2 * NQ * N * D + 2 * NQ * N * DV

@@ -24,6 +24,7 @@ NQ = 128
 CHUNKS = (0, 640, 1216, 1664, 2048)
 SPLIT = 384
 VS_ROW = 64
+KB_ROW = P - 1
 
 FLOPS = 2 * NQ * N * D + 2 * NQ * N * DV
 BYTES = 4 * (D * NQ + D * T + DV * T + 2 * T + 2 * NQ * DV) + 2 * P * (N // 16)
@@ -46,14 +47,14 @@ def tile_attend_x_norm_gate_topk_kernel(tc, qT, kT, vT, vs, kb, og, offs, out):
         gate_raw = keep.tile([P, DV], F32, name="gate_raw")
         ident = keep.tile([P, P], F32, name="ident")
 
-        nc.vector.memset(kb_pool[:], 0.0)
         nc.vector.memset(vs_pool[:], 0.0)
+        nc.vector.memset(kb_pool[:KB_ROW, :], 0.0)
         k_rows = kT.rearrange("(p t) n -> p t n", t=PACK)
         for t in range(PACK):
             nc.sync.dma_start(out=k_pool[t][:], in_=k_rows[:, t, :])
             if t == 0:
                 nc.sync.dma_start(offsets[:], offs)
-                nc.sync.dma_start(out=kb_pool[0:1, :], in_=kb[0:1, :])
+                nc.sync.dma_start(out=kb_pool[KB_ROW:, :], in_=kb[0:1, :])
             if t == 1:
                 nc.sync.dma_start(out=vs_pool[VS_ROW : VS_ROW + 1, :], in_=vs[0:1, :])
         nc.sync.dma_start(out=q_raw[:], in_=qT.rearrange("b (p t) q -> p (b t) q", t=PACK))
@@ -73,7 +74,7 @@ def tile_attend_x_norm_gate_topk_kernel(tc, qT, kT, vT, vs, kb, og, offs, out):
         for c in range(4):
             nc.tensor.transpose(kb_turned[:, c, :], kb_row[:, c:N:PACK], ident[:])
         kb_cols = keep.tile([P, 4], F32, name="kb_cols")
-        nc.scalar.copy(kb_cols[:], kb_turned[:, :, 0])
+        nc.scalar.copy(kb_cols[:], kb_turned[:, :, KB_ROW])
         kb_spread = psum.tile([P, 4, P], F32, name="kb_spread", tag="bank_b")
         for c in range(4):
             nc.tensor.transpose(kb_spread[:, c, :], kb_cols[:, c : c + 1].to_broadcast([P, P]), ident[:])

@@ -35,12 +35,15 @@ def tile_attend_x_norm_gate_topk_kernel(tc, qT, kT, vT, vs, kb, og, offs, out):
     with ExitStack() as ctx:
         keep = ctx.enter_context(tc.tile_pool(name="keep", bufs=1))
         late = ctx.enter_context(tc.tile_pool(name="late", bufs=1))
+        on_chunk = ctx.enter_context(tc.tile_pool(name="on_chunk", bufs=1))
         psum = ctx.enter_context(tc.psum_pool(name="psum", bufs=1))
 
         offsets = keep.tile([P, N // 16], U16, name="offsets")
         q_raw = late.tile([P, PACK, NQ], F32, name="q_raw", offset=8192 + 512, align_bytes=64)
         k_pool = [keep.tile([P, T], F32, name="k_pool%d" % t) for t in range(PACK)]
-        v0_pool = keep.tile([P, T], F32, name="v0_pool")
+        spans = list(zip(CHUNKS, CHUNKS[1:]))
+        v0_chunks = [keep.tile([P, b - a], F32, name="v0_chunk%d" % a) for a, b in spans[:-1]]
+        v0_chunks.append(on_chunk.tile([P, T - CHUNKS[-2]], F32, name="v0_last", offset=0))
         v1_pool = late.tile([P, T], F32, name="v1_pool", offset=0, align_bytes=64)
         kb_pool = keep.tile([P, T], F32, name="kb_pool")
         vs_pool = keep.tile([P, T], F32, name="vs_pool")
@@ -58,8 +61,8 @@ def tile_attend_x_norm_gate_topk_kernel(tc, qT, kT, vT, vs, kb, og, offs, out):
             if t == 1:
                 nc.sync.dma_start(out=vs_pool[VS_ROW : VS_ROW + 1, :], in_=vs[0:1, :])
         nc.sync.dma_start(out=q_raw[:], in_=qT.rearrange("b (p t) q -> p (b t) q", t=PACK))
-        for a, b in zip(CHUNKS, CHUNKS[1:]):
-            nc.sync.dma_start(out=v0_pool[:, a:b], in_=vT[0:P, a:b])
+        for chunk, (a, b) in zip(v0_chunks, spans):
+            nc.sync.dma_start(out=chunk[:], in_=vT[0:P, a:b])
         nc.sync.dma_start(out=v1_pool[:], in_=vT[P : 2 * P, :])
         nc.sync.dma_start(out=gate_raw[:], in_=og.rearrange("b q e -> (b q) e"))
         make_identity(nc, ident[:])
@@ -135,7 +138,7 @@ def tile_attend_x_norm_gate_topk_kernel(tc, qT, kT, vT, vs, kb, og, offs, out):
         v_codes = []
         v_scales = []
 
-        v_cast = keep.tile([P, T], BF16, name="v_cast", tag="v_cast_then_p")
+        v_cast = keep.tile([P, T], BF16, name="v_cast")
 
         v_picked = [keep.tile([P, N], BF16, name="v_picked%d" % b) for b in range(2)]
 
@@ -158,8 +161,8 @@ def tile_attend_x_norm_gate_topk_kernel(tc, qT, kT, vT, vs, kb, og, offs, out):
             v_codes.append(codes)
             v_scales.append(scales)
 
-        for a, b in zip(CHUNKS, CHUNKS[1:]):
-            nc.scalar.activation(v_cast[:, a:b], v0_pool[:, a:b], ACT.Copy)
+        for chunk, (a, b) in zip(v0_chunks, spans):
+            nc.scalar.activation(v_cast[:, a:b], chunk[:], ACT.Copy)
         nc.scalar.activation(v_picked[0][:, :SPLIT], v_cast[:].indirect(offsets[:, : SPLIT // 16]), ACT.Copy)
         for h in range(N // P):
             run = slice(h * P // PACK, (h + 1) * P // PACK)
@@ -172,12 +175,12 @@ def tile_attend_x_norm_gate_topk_kernel(tc, qT, kT, vT, vs, kb, og, offs, out):
         neg_m = keep.tile([P, 1], F32, name="neg_m")
         nc.vector.tensor_reduce(neg_m[:], s[:], mybir.AxisListType.X, MAX, negate=True)
 
-        nc.vector.tensor_copy(v_picked[0][:, SPLIT:], v0_pool[:].indirect(offsets[:, SPLIT // 16 :]))
+        nc.vector.tensor_copy(v_picked[0][:, SPLIT:], v_cast[:].indirect(offsets[:, SPLIT // 16 :]))
         nc.vector.tensor_copy(
             v_picked[1][:].rearrange("e (u s j) -> e s u j", u=2, j=2), v1_pool[:].indirect(offsets[:])
         )
 
-        p = keep.tile([P, PACK, P], F32, name="p", tag="v_cast_then_p")
+        p = on_chunk.tile([P, PACK, P], F32, name="p", offset=0)
         part = [keep.tile([P, 1], F32, name="part%d" % u) for u in range(2)]
         for u in range(2):
             nc.scalar.activation(

@@ -21,8 +21,9 @@ T = 2048
 D = 512
 DV = 256
 NQ = 128
-CHUNKS = (0, 640, 1216, 1664, 2048)
-SPLIT = 384
+K_SPLIT = 384
+V0_SPLIT = 256
+V1_SPLIT = 320
 VS_ROW = 64
 KB_ROW = P - 1
 
@@ -34,20 +35,26 @@ def tile_attend_x_norm_gate_topk_kernel(tc, qT, kT, vT, vs, kb, og, offs, out):
     nc = tc.nc
     with ExitStack() as ctx:
         keep = ctx.enter_context(tc.tile_pool(name="keep", bufs=1))
-        late = ctx.enter_context(tc.tile_pool(name="late", bufs=1))
-        on_chunk = ctx.enter_context(tc.tile_pool(name="on_chunk", bufs=1))
+        on_v1 = ctx.enter_context(tc.tile_pool(name="on_v1", bufs=1))
+        on_q = ctx.enter_context(tc.tile_pool(name="on_q", bufs=1))
+        on_picked = ctx.enter_context(tc.tile_pool(name="on_picked", bufs=1))
+        on_grouped = ctx.enter_context(tc.tile_pool(name="on_grouped", bufs=1))
         psum = ctx.enter_context(tc.psum_pool(name="psum", bufs=1))
 
+        def slots(a, b):
+            return offsets[:, a // 16 : b // 16]
+
         offsets = keep.tile([P, N // 16], U16, name="offsets")
-        q_raw = late.tile([P, PACK, NQ], F32, name="q_raw", offset=8192 + 512, align_bytes=64)
+        q_raw = on_q.tile([P, PACK, NQ], F32, name="q_raw", offset=0, align_bytes=64)
         k_pool = [keep.tile([P, T], F32, name="k_pool%d" % t) for t in range(PACK)]
-        spans = list(zip(CHUNKS, CHUNKS[1:]))
-        v0_chunks = [keep.tile([P, b - a], F32, name="v0_chunk%d" % a) for a, b in spans[:-1]]
-        v0_chunks.append(on_chunk.tile([P, T - CHUNKS[-2]], F32, name="v0_last", offset=0))
-        v1_pool = late.tile([P, T], F32, name="v1_pool", offset=0, align_bytes=64)
+        v0_pool = keep.tile([P, T], F32, name="v0_pool")
+        v1_pool = on_v1.tile([P, T], F32, name="v1_pool", offset=0, align_bytes=64)
         kb_pool = keep.tile([P, T], F32, name="kb_pool")
         vs_pool = keep.tile([P, T], F32, name="vs_pool")
-        gate_raw = keep.tile([P, DV], F32, name="gate_raw")
+        gate_raw = [
+            keep.tile([P, P], F32, name="gate_raw0"),
+            keep.tile([P, P], F32, name="gate_raw1"),
+        ]
         ident = keep.tile([P, P], F32, name="ident")
 
         nc.vector.memset(vs_pool[:], 0.0)
@@ -59,16 +66,17 @@ def tile_attend_x_norm_gate_topk_kernel(tc, qT, kT, vT, vs, kb, og, offs, out):
                 nc.sync.dma_start(offsets[:], offs)
                 nc.sync.dma_start(out=kb_pool[KB_ROW:, :], in_=kb[0:1, :])
             if t == 1:
-                nc.sync.dma_start(out=vs_pool[VS_ROW : VS_ROW + 1, :], in_=vs[0:1, :])
+                for a in (0, T // 2):
+                    nc.sync.dma_start(out=vs_pool[VS_ROW : VS_ROW + 1, a : a + T // 2], in_=vs[0:1, a : a + T // 2])
         nc.sync.dma_start(out=q_raw[:], in_=qT.rearrange("b (p t) q -> p (b t) q", t=PACK))
-        for chunk, (a, b) in zip(v0_chunks, spans):
-            nc.sync.dma_start(out=chunk[:], in_=vT[0:P, a:b])
+        nc.sync.dma_start(out=v0_pool[:], in_=vT[0:P, :])
         nc.sync.dma_start(out=v1_pool[:], in_=vT[P : 2 * P, :])
-        nc.sync.dma_start(out=gate_raw[:], in_=og.rearrange("b q e -> (b q) e"))
+        og_rows = og.rearrange("b q e -> (b q) e")
+        for b in range(2):
+            nc.sync.dma_start(out=gate_raw[b][:], in_=og_rows[:, b * P : (b + 1) * P])
         make_identity(nc, ident[:])
 
         k_grouped = keep.tile([P, N, PACK], BF16, name="k_grouped", align_bytes=64)
-
         k_low = keep.tile([P, 2, N], BF16, name="k_low")
         nc.vector.tensor_copy(k_low[:, 0, :], k_pool[0][:].indirect(offsets[:]))
         kb_row = keep.tile([P, N], F32, name="kb_row")
@@ -81,8 +89,21 @@ def tile_attend_x_norm_gate_topk_kernel(tc, qT, kT, vT, vs, kb, og, offs, out):
         kb_spread = psum.tile([P, 4, P], F32, name="kb_spread", tag="bank_b")
         for c in range(4):
             nc.tensor.transpose(kb_spread[:, c, :], kb_cols[:, c : c + 1].to_broadcast([P, P]), ident[:])
-        kb_all = keep.tile([P, N], F32, name="kb_all")
-        nc.scalar.copy(kb_all[:], kb_spread[:].rearrange("p c q -> p (c q)"))
+        order = (3, 0, 1, 2)
+        first_kb = P + V0_SPLIT // PACK
+        shared = keep.tile([P, first_kb + N], F32, name="shared", align_bytes=64)
+        run = P // PACK
+
+        def kb_piece(h):
+            place = first_kb + P * ((h - order[-1]) % 4)
+            return shared[:, place : place + P].rearrange("q (t s) -> q t s", t=PACK)
+
+        for h0 in (0, 2):
+            place = first_kb + P * ((h0 - order[-1]) % 4)
+            nc.scalar.copy(
+                shared[:, place : place + 2 * P].rearrange("q (h t s) -> q h t s", h=2, t=PACK),
+                kb_spread[:, :, h0 * run : (h0 + 2) * run].rearrange("q t (h s) -> q h t s", h=2),
+            )
 
         nc.vector.tensor_copy(k_low[:, 1, :], k_pool[1][:].indirect(offsets[:]))
         nc.scalar.copy(k_grouped[:, :, 0:2], k_low[:].rearrange("p t n -> p n t"))
@@ -94,93 +115,61 @@ def tile_attend_x_norm_gate_topk_kernel(tc, qT, kT, vT, vs, kb, og, offs, out):
         vs_cols = keep.tile([P, PACK], F32, name="vs_cols")
         nc.scalar.copy(vs_cols[:], vs_turned[:, :, VS_ROW])
 
-        nc.vector.tensor_copy(k_grouped[:, :, 2], k_pool[2][:].indirect(offsets[:]))
-        half = N // 2
-        for h in range(2):
-            nc.vector.tensor_copy(
-                k_grouped[:, h * half : (h + 1) * half, 3],
-                k_pool[3][:].indirect(offsets[:, h * half // 16 : (h + 1) * half // 16]),
-            )
+        for t in (2, 3):
+            nc.vector.tensor_copy(k_grouped[:, :K_SPLIT, t], k_pool[t][:].indirect(slots(0, K_SPLIT)))
+            nc.scalar.activation(k_grouped[:, K_SPLIT:, t], k_pool[t][:].indirect(slots(K_SPLIT, N)), ACT.Copy)
+
         q_grouped = keep.tile([P, NQ, PACK], BF16, name="q_grouped", align_bytes=64)
         q_codes = keep.tile([P, NQ], U32, name="q_codes", align_bytes=64)
         q_scales = keep.tile([P, NQ], U8, name="q_scales", align_bytes=64)
         nc.scalar.copy(q_grouped[:], q_raw[:].rearrange("p t q -> p q t"))
-        nc.vector.quantize_mx(
-            out=q_codes[:].bitcast(FP8X4), scales=q_scales[:], in_=q_grouped[:].rearrange("p q t -> p (q t)")
-        )
-
-        k_codes = [
-            late.tile([P, P], U32, name="k_codes%d" % h, offset=8192 + 512 * h, align_bytes=64) for h in range(N // P)
-        ]
+        k_codes = [on_q.tile([P, P], U32, name="k_codes%d" % h, offset=512 * h, align_bytes=64) for h in range(3)]
+        k_codes.append(keep.tile([P, P], U32, name="k_codes3", align_bytes=64))
         k_scales = keep.tile([P, N], U8, name="k_scales", align_bytes=64)
         k_flat = k_grouped[:].rearrange("p n t -> p (n t)")
-        for h in range(N // P):
+
+        def quantize_keys(h):
             nc.vector.quantize_mx(
                 out=k_codes[h][:].bitcast(FP8X4),
                 scales=k_scales[:, h * P : (h + 1) * P],
                 in_=k_flat[:, h * P * PACK : (h + 1) * P * PACK],
             )
-        score_banks = ["bank_s0", "bank_s1", "bank_s2", "bank_p"]
+
+        quantize_keys(order[0])
+        nc.vector.quantize_mx(
+            out=q_codes[:].bitcast(FP8X4), scales=q_scales[:], in_=q_grouped[:].rearrange("p q t -> p (q t)")
+        )
+        for h in order[1:]:
+            quantize_keys(h)
+        score_banks = ["bank_s0", "bank_s1", "bank_p", "bank_s2"]
         scores = [psum.tile([P, P], F32, name="scores%d" % h, tag=score_banks[h]) for h in range(N // P)]
         s = keep.tile([P, N], F32, name="s")
-        for h in range(N // P):
-            cols = slice(h * P, (h + 1) * P)
+        for h in order:
             nc.tensor.matmul_mx(
                 out=scores[h][:],
                 lhsT=q_codes[:].bitcast(FP8X4),
                 lhsT_scale=q_scales[:],
                 rhs=k_codes[h][:].bitcast(FP8X4),
-                rhs_scale=k_scales[:, cols],
+                rhs_scale=k_scales[:, h * P : (h + 1) * P],
                 start=True,
                 stop=True,
             )
-        v_grouped = []
-        v_codes = []
-        v_scales = []
 
-        v_cast = keep.tile([P, T], BF16, name="v_cast")
-
-        v_picked = [keep.tile([P, N], BF16, name="v_picked%d" % b) for b in range(2)]
-
-        def turn_values(b):
-            words = v_picked[b][:].bitcast(F32)
-            turned = psum.tile([P, 2, P], F32, name="v_turned%d" % b, tag="bank_v%d" % b)
-            for u in range(2):
-                picked = words[:, u : N // 2 : 2] if b == 0 else words[:, u * P : (u + 1) * P]
-                nc.tensor.transpose(turned[:, u, :], picked, ident[:])
-            grouped = keep.tile([P, P * PACK], BF16, name="v_grouped%d" % b, align_bytes=64)
-            nc.scalar.copy(
-                grouped[:].bitcast(F32).rearrange("s (e u) -> s e u", u=2), turned[:].rearrange("s u e -> s e u")
-            )
-            v_grouped.append(grouped)
-
-        def quantize_values(b):
-            codes = late.tile([P, P], U32, name="v_codes%d" % b, offset=2048 + 512 * b, align_bytes=64)
-            scales = keep.tile([P, P], U8, name="v_scales%d" % b, align_bytes=64)
-            nc.vector.quantize_mx(out=codes[:].bitcast(FP8X4), scales=scales[:], in_=v_grouped[b][:])
-            v_codes.append(codes)
-            v_scales.append(scales)
-
-        for chunk, (a, b) in zip(v0_chunks, spans):
-            nc.scalar.activation(v_cast[:, a:b], chunk[:], ACT.Copy)
-        nc.scalar.activation(v_picked[0][:, :SPLIT], v_cast[:].indirect(offsets[:, : SPLIT // 16]), ACT.Copy)
-        for h in range(N // P):
-            run = slice(h * P // PACK, (h + 1) * P // PACK)
+        v0_dealt = shared[:, : N // 2].bitcast(BF16).rearrange("e (u s j) -> e s u j", u=2, j=2)
+        v1_picked = on_picked.tile([P, N], BF16, name="v1_picked", offset=0, align_bytes=64)
+        nc.scalar.activation(v0_dealt[:, : V0_SPLIT // PACK], v0_pool[:].indirect(slots(0, V0_SPLIT)), ACT.Copy)
+        for h in order:
             nc.vector.tensor_tensor(
-                s[:].rearrange("q (t s) -> q t s", t=PACK)[:, :, run],
-                kb_all[:].rearrange("q (t s) -> q t s", t=PACK)[:, :, run],
+                s[:].rearrange("q (t s) -> q t s", t=PACK)[:, :, h * run : (h + 1) * run],
+                kb_piece(h),
                 scores[h][:].rearrange("q (s t) -> q t s", t=PACK),
                 ADD,
             )
         neg_m = keep.tile([P, 1], F32, name="neg_m")
         nc.vector.tensor_reduce(neg_m[:], s[:], mybir.AxisListType.X, MAX, negate=True)
+        nc.vector.tensor_copy(v0_dealt[:, V0_SPLIT // PACK :], v0_pool[:].indirect(slots(V0_SPLIT, N)))
 
-        nc.vector.tensor_copy(v_picked[0][:, SPLIT:], v_cast[:].indirect(offsets[:, SPLIT // 16 :]))
-        nc.vector.tensor_copy(
-            v_picked[1][:].rearrange("e (u s j) -> e s u j", u=2, j=2), v1_pool[:].indirect(offsets[:])
-        )
-
-        p = on_chunk.tile([P, PACK, P], F32, name="p", offset=0)
+        p = keep.tile([P, PACK, P], F32, name="p")
         part = [keep.tile([P, 1], F32, name="part%d" % u) for u in range(2)]
         for u in range(2):
             nc.scalar.activation(
@@ -190,13 +179,39 @@ def tile_attend_x_norm_gate_topk_kernel(tc, qT, kT, vT, vs, kb, og, offs, out):
                 bias=neg_m[:],
                 accum_out=part[u][:],
             )
-        total = keep.tile([P, 1], F32, name="total")
-        nc.scalar.activation(total[:], part[0][:], ACT.Identity, bias=part[1][:])
-        turn_values(0)
+        dealt = v1_picked[:].rearrange("e (u s j) -> e s u j", u=2, j=2)
+        nc.vector.tensor_copy(dealt[:, : V1_SPLIT // PACK], v1_pool[:].indirect(slots(0, V1_SPLIT)))
+        nc.scalar.activation(dealt[:, V1_SPLIT // PACK :], v1_pool[:].indirect(slots(V1_SPLIT, N)), ACT.Copy)
+
+        v0_turned = psum.tile([P, 2, P], F32, name="v0_turned", tag="bank_v0")
+        for u in range(2):
+            nc.tensor.transpose(v0_turned[:, u, :], shared[:, u * P : (u + 1) * P], ident[:])
         p_turned = psum.tile([P, PACK, NQ], F32, name="p_turned", tag="bank_p")
         for t in range(PACK):
             nc.tensor.transpose(p_turned[:, t, :], p[:, t, :], ident[:])
-        w = late.tile([P, NQ, PACK], BF16, name="w", offset=0, align_bytes=64)
+        v1_turned = psum.tile([P, 2, P], F32, name="v1_turned", tag="bank_v1")
+        for u in range(2):
+            nc.tensor.transpose(v1_turned[:, u, :], v1_picked[:].bitcast(F32)[:, u * P : (u + 1) * P], ident[:])
+
+        gate_tanh = keep.tile([P, DV], F32, name="gate_tanh")
+        nc.scalar.activation(gate_tanh[:, :P], gate_raw[0][:], ACT.Tanh, scale=0.5)
+        nc.scalar.activation(gate_tanh[:, P:], gate_raw[1][:], ACT.Tanh, scale=0.5)
+        total = on_v1.tile([P, 1], F32, name="total", offset=2048, align_bytes=64)
+        nc.scalar.activation(total[:], part[0][:], ACT.Identity, bias=part[1][:])
+        v_grouped = [
+            on_v1.tile([P, N], BF16, name="v_grouped0", offset=1024, align_bytes=64),
+            on_grouped.tile([P, N], BF16, name="v_grouped1", offset=0, align_bytes=64),
+        ]
+        for b, turned in enumerate((v0_turned, v1_turned)):
+            nc.scalar.copy(
+                v_grouped[b][:].bitcast(F32).rearrange("s (e u) -> s e u", u=2), turned[:].rearrange("s u e -> s e u")
+            )
+        gate = on_picked.tile([P, DV], F32, name="gate", offset=0, align_bytes=64)
+        for b in range(2):
+            cols = slice(b * P, (b + 1) * P)
+            nc.scalar.activation(gate[:, cols], gate_tanh[:, cols], ACT.Copy, bias=0.5, scale=0.5)
+
+        w = on_v1.tile([P, NQ, PACK], BF16, name="w", offset=0, align_bytes=64)
         w_codes = keep.tile([P, NQ], U32, name="w_codes", align_bytes=64)
         w_scales = keep.tile([P, NQ], U8, name="w_scales", align_bytes=64)
         q_halves = [slice(0, NQ // 2), slice(NQ // 2, NQ)]
@@ -207,9 +222,10 @@ def tile_attend_x_norm_gate_topk_kernel(tc, qT, kT, vT, vs, kb, og, offs, out):
                 vs_cols[:].unsqueeze(1).to_broadcast([P, NQ // 2, PACK]),
                 MULT,
             )
-        turn_values(1)
-        quantize_values(0)
-        inv_total = late.tile([P, 1], F32, name="inv_total", offset=4096)
+        v_codes = [keep.tile([P, P], U32, name="v_codes%d" % b, align_bytes=64) for b in range(2)]
+        v_scales = [keep.tile([P, P], U8, name="v_scales%d" % b, align_bytes=64) for b in range(2)]
+        nc.vector.quantize_mx(out=v_codes[0][:].bitcast(FP8X4), scales=v_scales[0][:], in_=v_grouped[0][:])
+        inv_total = keep.tile([P, 1], F32, name="inv_total")
         nc.vector.reciprocal(inv_total[:], total[:])
         for rows in q_halves:
             nc.vector.quantize_mx(
@@ -217,14 +233,12 @@ def tile_attend_x_norm_gate_topk_kernel(tc, qT, kT, vT, vs, kb, og, offs, out):
                 scales=w_scales[:, rows],
                 in_=w[:, rows, :].rearrange("p q t -> p (q t)"),
             )
-        quantize_values(1)
+        nc.vector.quantize_mx(out=v_codes[1][:].bitcast(FP8X4), scales=v_scales[1][:], in_=v_grouped[1][:])
 
-        gate_tanh = keep.tile([P, DV], F32, name="gate_tanh")
-        gate = keep.tile([P, DV], F32, name="gate")
-        nc.scalar.activation(gate_tanh[:], gate_raw[:], ACT.Tanh, scale=0.5)
-        nc.scalar.activation(gate[:], gate_tanh[:], ACT.Copy, bias=0.5, scale=0.5)
-
-        result = keep.tile([P, DV], F32, name="result")
+        results = [
+            on_grouped.tile([P, P], F32, name="result0", offset=0, align_bytes=64),
+            keep.tile([P, P], F32, name="result1"),
+        ]
         out_rows = out.rearrange("b q e -> (b q) e")
         y = []
         for b in range(2):
@@ -241,5 +255,7 @@ def tile_attend_x_norm_gate_topk_kernel(tc, qT, kT, vT, vs, kb, og, offs, out):
             y.append(acc)
         for b in range(2):
             cols = slice(b * P, (b + 1) * P)
-            nc.vector.scalar_tensor_tensor(result[:, cols], y[b][:], inv_total[:], gate[:, cols], MULT, MULT)
-            nc.sync.dma_start(out=out_rows[:, cols], in_=result[:, cols])
+            nc.vector.scalar_tensor_tensor(results[b][:], y[b][:], inv_total[:], gate[:, cols], MULT, MULT)
+            width = P // 2 if b == 0 else P
+            for a in range(0, P, width):
+                nc.sync.dma_start(out=out_rows[:, b * P + a : b * P + a + width], in_=results[b][:, a : a + width])

@@ -64,7 +64,8 @@ def tile_attend_x_norm_gate_topk_kernel(tc, qT, kT, vT, vs, kb, og, offs, out):
             nc.sync.dma_start(out=k_pool[t][:], in_=k_rows[:, t, :])
             if t == 0:
                 nc.sync.dma_start(offsets[:], offs)
-                nc.sync.dma_start(out=kb_pool[KB_ROW:, :], in_=kb[0:1, :])
+                for a in (0, T // 2):
+                    nc.sync.dma_start(out=kb_pool[KB_ROW:, a : a + T // 2], in_=kb[0:1, a : a + T // 2])
             if t == 1:
                 for a in (0, T // 2):
                     nc.sync.dma_start(out=vs_pool[VS_ROW : VS_ROW + 1, a : a + T // 2], in_=vs[0:1, a : a + T // 2])
@@ -95,15 +96,14 @@ def tile_attend_x_norm_gate_topk_kernel(tc, qT, kT, vT, vs, kb, og, offs, out):
         run = P // PACK
 
         def kb_piece(h):
-            place = first_kb + P * ((h - order[-1]) % 4)
+            place = first_kb + P * ((h - order[-2]) % 4)
             return shared[:, place : place + P].rearrange("q (t s) -> q t s", t=PACK)
 
-        for h0 in (0, 2):
-            place = first_kb + P * ((h0 - order[-1]) % 4)
-            nc.scalar.copy(
-                shared[:, place : place + 2 * P].rearrange("q (h t s) -> q h t s", h=2, t=PACK),
-                kb_spread[:, :, h0 * run : (h0 + 2) * run].rearrange("q t (h s) -> q h t s", h=2),
-            )
+        nc.scalar.copy(kb_piece(0), kb_spread[:, :, :run])
+        nc.scalar.copy(
+            shared[:, first_kb : first_kb + 3 * P].rearrange("q (h t s) -> q h t s", h=3, t=PACK),
+            kb_spread[:, :, run:].rearrange("q t (h s) -> q h t s", h=3),
+        )
 
         nc.vector.tensor_copy(k_low[:, 1, :], k_pool[1][:].indirect(offsets[:]))
         nc.scalar.copy(k_grouped[:, :, 0:2], k_low[:].rearrange("p t n -> p n t"))
@@ -112,8 +112,6 @@ def tile_attend_x_norm_gate_topk_kernel(tc, qT, kT, vT, vs, kb, og, offs, out):
         vs_turned = psum.tile([P, PACK, P], F32, name="vs_turned", tag="bank_a")
         for t in range(PACK):
             nc.tensor.transpose(vs_turned[:, t, :], vs_row[:, t:N:PACK], ident[:])
-        vs_cols = keep.tile([P, PACK], F32, name="vs_cols")
-        nc.scalar.copy(vs_cols[:], vs_turned[:, :, VS_ROW])
 
         for t in (2, 3):
             nc.vector.tensor_copy(k_grouped[:, :K_SPLIT, t], k_pool[t][:].indirect(slots(0, K_SPLIT)))
@@ -170,25 +168,23 @@ def tile_attend_x_norm_gate_topk_kernel(tc, qT, kT, vT, vs, kb, og, offs, out):
         nc.vector.tensor_copy(v0_dealt[:, V0_SPLIT // PACK :], v0_pool[:].indirect(slots(V0_SPLIT, N)))
 
         p = keep.tile([P, PACK, P], F32, name="p")
-        part = [keep.tile([P, 1], F32, name="part%d" % u) for u in range(2)]
-        for u in range(2):
+        part = keep.tile([P, PACK], F32, name="part")
+        for t in range(PACK):
             nc.scalar.activation(
-                p[:, 2 * u : 2 * u + 2, :].rearrange("q r s -> q (r s)"),
-                s[:, 2 * u * P : (2 * u + 2) * P],
-                ACT.Exp,
-                bias=neg_m[:],
-                accum_out=part[u][:],
+                p[:, t, :], s[:, t * P : (t + 1) * P], ACT.Exp, bias=neg_m[:], accum_out=part[:, t : t + 1]
             )
+        vs_cols = s[:, 2 * P : 2 * P + PACK]
+        nc.scalar.copy(vs_cols, vs_turned[:, :, VS_ROW])
         dealt = v1_picked[:].rearrange("e (u s j) -> e s u j", u=2, j=2)
         nc.vector.tensor_copy(dealt[:, : V1_SPLIT // PACK], v1_pool[:].indirect(slots(0, V1_SPLIT)))
         nc.scalar.activation(dealt[:, V1_SPLIT // PACK :], v1_pool[:].indirect(slots(V1_SPLIT, N)), ACT.Copy)
 
-        v0_turned = psum.tile([P, 2, P], F32, name="v0_turned", tag="bank_v0")
-        for u in range(2):
-            nc.tensor.transpose(v0_turned[:, u, :], shared[:, u * P : (u + 1) * P], ident[:])
         p_turned = psum.tile([P, PACK, NQ], F32, name="p_turned", tag="bank_p")
         for t in range(PACK):
             nc.tensor.transpose(p_turned[:, t, :], p[:, t, :], ident[:])
+        v0_turned = psum.tile([P, 2, P], F32, name="v0_turned", tag="bank_a")
+        for u in range(2):
+            nc.tensor.transpose(v0_turned[:, u, :], shared[:, u * P : (u + 1) * P], ident[:])
         v1_turned = psum.tile([P, 2, P], F32, name="v1_turned", tag="bank_v1")
         for u in range(2):
             nc.tensor.transpose(v1_turned[:, u, :], v1_picked[:].bitcast(F32)[:, u * P : (u + 1) * P], ident[:])
@@ -197,7 +193,7 @@ def tile_attend_x_norm_gate_topk_kernel(tc, qT, kT, vT, vs, kb, og, offs, out):
         nc.scalar.activation(gate_tanh[:, :P], gate_raw[0][:], ACT.Tanh, scale=0.5)
         nc.scalar.activation(gate_tanh[:, P:], gate_raw[1][:], ACT.Tanh, scale=0.5)
         total = on_v1.tile([P, 1], F32, name="total", offset=2048, align_bytes=64)
-        nc.scalar.activation(total[:], part[0][:], ACT.Identity, bias=part[1][:])
+        nc.scalar.activation(part[:], part[:], ACT.Copy, accum_out=total[:])
         v_grouped = [
             on_v1.tile([P, N], BF16, name="v_grouped0", offset=1024, align_bytes=64),
             on_grouped.tile([P, N], BF16, name="v_grouped1", offset=0, align_bytes=64),
@@ -219,7 +215,7 @@ def tile_attend_x_norm_gate_topk_kernel(tc, qT, kT, vT, vs, kb, og, offs, out):
             nc.vector.tensor_tensor(
                 w[:, rows, :],
                 p_turned[:].rearrange("s t q -> s q t")[:, rows, :],
-                vs_cols[:].unsqueeze(1).to_broadcast([P, NQ // 2, PACK]),
+                vs_cols.unsqueeze(1).to_broadcast([P, NQ // 2, PACK]),
                 MULT,
             )
         v_codes = [keep.tile([P, P], U32, name="v_codes%d" % b, align_bytes=64) for b in range(2)]
@@ -242,7 +238,7 @@ def tile_attend_x_norm_gate_topk_kernel(tc, qT, kT, vT, vs, kb, og, offs, out):
         out_rows = out.rearrange("b q e -> (b q) e")
         y = []
         for b in range(2):
-            acc = psum.tile([P, P], F32, name="y%d" % b, tag="bank_%s" % "ab"[b])
+            acc = psum.tile([P, P], F32, name="y%d" % b, tag=("bank_y", "bank_b")[b])
             nc.tensor.matmul_mx(
                 out=acc[:],
                 lhsT=w_codes[:].bitcast(FP8X4),
@@ -256,6 +252,4 @@ def tile_attend_x_norm_gate_topk_kernel(tc, qT, kT, vT, vs, kb, og, offs, out):
         for b in range(2):
             cols = slice(b * P, (b + 1) * P)
             nc.vector.scalar_tensor_tensor(results[b][:], y[b][:], inv_total[:], gate[:, cols], MULT, MULT)
-            width = P // 2 if b == 0 else P
-            for a in range(0, P, width):
-                nc.sync.dma_start(out=out_rows[:, b * P + a : b * P + a + width], in_=results[b][:, a : a + width])
+            nc.sync.dma_start(out=out_rows[:, cols], in_=results[b][:])

@@ -64,17 +64,16 @@ def tile_attend_x_norm_gate_topk_kernel(tc, qT, kT, vT, vs, kb, og, offs, out):
             nc.sync.dma_start(out=k_pool[t][:], in_=k_rows[:, t, :])
             if t == 0:
                 nc.sync.dma_start(offsets[:], offs)
-                for a in (0, T // 2):
-                    nc.sync.dma_start(out=kb_pool[KB_ROW:, a : a + T // 2], in_=kb[0:1, a : a + T // 2])
+                nc.sync.dma_start(out=kb_pool[KB_ROW:, :], in_=kb[0:1, :])
             if t == 1:
-                for a in (0, T // 2):
-                    nc.sync.dma_start(out=vs_pool[VS_ROW : VS_ROW + 1, a : a + T // 2], in_=vs[0:1, a : a + T // 2])
+                nc.sync.dma_start(out=vs_pool[VS_ROW : VS_ROW + 1, :], in_=vs[0:1, :])
         nc.sync.dma_start(out=q_raw[:], in_=qT.rearrange("b (p t) q -> p (b t) q", t=PACK))
         nc.sync.dma_start(out=v0_pool[:], in_=vT[0:P, :])
         nc.sync.dma_start(out=v1_pool[:], in_=vT[P : 2 * P, :])
         og_rows = og.rearrange("b q e -> (b q) e")
-        for b in range(2):
-            nc.sync.dma_start(out=gate_raw[b][:], in_=og_rows[:, b * P : (b + 1) * P])
+        nc.sync.dma_start(out=gate_raw[0][:], in_=og_rows[:, :P])
+        for a, b in ((0, 64), (64, 96), (96, P)):
+            nc.sync.dma_start(out=gate_raw[1][a:b, :], in_=og_rows[a:b, P:])
         make_identity(nc, ident[:])
 
         k_grouped = keep.tile([P, N, PACK], BF16, name="k_grouped", align_bytes=64)

@@ -23,7 +23,7 @@ DV = 256
 NQ = 128
 K_SPLIT = 384
 V0_SPLIT = 256
-V1_SPLIT = 320
+V1_SPLIT = 256
 VS_ROW = 64
 KB_ROW = P - 1
 

@@ -23,7 +23,7 @@ DV = 256
 NQ = 128
 K_SPLIT = 384
 V0_SPLIT = 256
-V1_SPLIT = 256
+V1_SPLIT = 288
 VS_ROW = 64
 KB_ROW = P - 1
 
@@ -197,9 +197,11 @@ def tile_attend_x_norm_gate_topk_kernel(tc, qT, kT, vT, vs, kb, og, offs, out):
             on_v1.tile([P, N], BF16, name="v_grouped0", offset=1024, align_bytes=64),
             on_grouped.tile([P, N], BF16, name="v_grouped1", offset=0, align_bytes=64),
         ]
-        for b, turned in enumerate((v0_turned, v1_turned)):
+        pieces = ((0, 0, P), (1, 0, P // 2), (1, P // 2, P))
+        for b, a, z in pieces:
             nc.scalar.copy(
-                v_grouped[b][:].bitcast(F32).rearrange("s (e u) -> s e u", u=2), turned[:].rearrange("s u e -> s e u")
+                v_grouped[b][:].bitcast(F32).rearrange("s (e u) -> s e u", u=2)[:, a:z, :],
+                (v0_turned, v1_turned)[b][:].rearrange("s u e -> s e u")[:, a:z, :],
             )
         gate = on_picked.tile([P, DV], F32, name="gate", offset=0, align_bytes=64)
         for b in range(2):
@@ -217,18 +219,24 @@ def tile_attend_x_norm_gate_topk_kernel(tc, qT, kT, vT, vs, kb, og, offs, out):
                 vs_cols.unsqueeze(1).to_broadcast([P, NQ // 2, PACK]),
                 MULT,
             )
+        inv_total = keep.tile([P, 1], F32, name="inv_total")
         v_codes = [keep.tile([P, P], U32, name="v_codes%d" % b, align_bytes=64) for b in range(2)]
         v_scales = [keep.tile([P, P], U8, name="v_scales%d" % b, align_bytes=64) for b in range(2)]
-        nc.vector.quantize_mx(out=v_codes[0][:].bitcast(FP8X4), scales=v_scales[0][:], in_=v_grouped[0][:])
-        inv_total = keep.tile([P, 1], F32, name="inv_total")
-        nc.vector.reciprocal(inv_total[:], total[:])
         for rows in q_halves:
             nc.vector.quantize_mx(
                 out=w_codes[:, rows].bitcast(FP8X4),
                 scales=w_scales[:, rows],
                 in_=w[:, rows, :].rearrange("p q t -> p (q t)"),
             )
-        nc.vector.quantize_mx(out=v_codes[1][:].bitcast(FP8X4), scales=v_scales[1][:], in_=v_grouped[1][:])
+            if rows.start == 0:
+                nc.vector.reciprocal(inv_total[:], total[:])
+        nc.vector.quantize_mx(out=v_codes[0][:].bitcast(FP8X4), scales=v_scales[0][:], in_=v_grouped[0][:])
+        for b, a, z in pieces[1:]:
+            nc.vector.quantize_mx(
+                out=v_codes[b][:, a:z].bitcast(FP8X4),
+                scales=v_scales[b][:, a:z],
+                in_=v_grouped[b][:, a * PACK : z * PACK],
+            )
 
         results = [
             on_grouped.tile([P, P], F32, name="result0", offset=0, align_bytes=64),
@@ -236,19 +244,20 @@ def tile_attend_x_norm_gate_topk_kernel(tc, qT, kT, vT, vs, kb, og, offs, out):
         ]
         out_rows = out.rearrange("b q e -> (b q) e")
         y = []
-        for b in range(2):
-            acc = psum.tile([P, P], F32, name="y%d" % b, tag=("bank_y", "bank_b")[b])
+        for (b, a, z), bank in zip(pieces, ("bank_y", "bank_b", "bank_s0")):
+            acc = psum.tile([P, z - a], F32, name="y%d_%d" % (b, a), tag=bank)
             nc.tensor.matmul_mx(
                 out=acc[:],
                 lhsT=w_codes[:].bitcast(FP8X4),
                 lhsT_scale=w_scales[:],
-                rhs=v_codes[b][:].bitcast(FP8X4),
-                rhs_scale=v_scales[b][:],
+                rhs=v_codes[b][:, a:z].bitcast(FP8X4),
+                rhs_scale=v_scales[b][:, a:z],
                 start=True,
                 stop=True,
             )
             y.append(acc)
-        for b in range(2):
-            cols = slice(b * P, (b + 1) * P)
-            nc.vector.scalar_tensor_tensor(results[b][:], y[b][:], inv_total[:], gate[:, cols], MULT, MULT)
-            nc.sync.dma_start(out=out_rows[:, cols], in_=results[b][:])
+        for (b, a, z), acc in zip(pieces, y):
+            cols = slice(b * P + a, b * P + z)
+            nc.vector.scalar_tensor_tensor(results[b][:, a:z], acc[:], inv_total[:], gate[:, cols], MULT, MULT)
+            if z == P:
+                nc.sync.dma_start(out=out_rows[:, b * P : (b + 1) * P], in_=results[b][:])

from contextlib import ExitStack

import concourse.mybir as mybir
from concourse.masks import make_identity

F32 = mybir.dt.float32
BF16 = mybir.dt.bfloat16
U32 = mybir.dt.uint32
U16 = mybir.dt.uint16
U8 = mybir.dt.uint8
FP8X4 = mybir.dt.float8_e4m3fn_x4
ADD = mybir.AluOpType.add
MULT = mybir.AluOpType.mult
MAX = mybir.AluOpType.max
ACT = mybir.ActivationFunctionType

P = 128
PACK = 4
N = 512
T = 2048
D = 512
DV = 256
NQ = 128
K_SPLIT = 384
V0_SPLIT = 256
V1_SPLIT = 288
VS_ROW = 64
KB_ROW = P - 1

FLOPS = 2 * NQ * N * D + 2 * NQ * N * DV
BYTES = 4 * (D * NQ + D * T + DV * T + 2 * T + 2 * NQ * DV) + 2 * P * (N // 16)


def tile_attend_x_norm_gate_topk_kernel(tc, qT, kT, vT, vs, kb, og, offs, out):
    nc = tc.nc
    with ExitStack() as ctx:
        keep = ctx.enter_context(tc.tile_pool(name="keep", bufs=1))
        on_v1 = ctx.enter_context(tc.tile_pool(name="on_v1", bufs=1))
        on_q = ctx.enter_context(tc.tile_pool(name="on_q", bufs=1))
        on_picked = ctx.enter_context(tc.tile_pool(name="on_picked", bufs=1))
        on_grouped = ctx.enter_context(tc.tile_pool(name="on_grouped", bufs=1))
        psum = ctx.enter_context(tc.psum_pool(name="psum", bufs=1))

        def slots(a, b):
            return offsets[:, a // 16 : b // 16]

        offsets = keep.tile([P, N // 16], U16, name="offsets")
        q_raw = on_q.tile([P, PACK, NQ], F32, name="q_raw", offset=0, align_bytes=64)
        k_pool = [keep.tile([P, T], F32, name="k_pool%d" % t) for t in range(PACK)]
        v0_pool = keep.tile([P, T], F32, name="v0_pool")
        v1_pool = on_v1.tile([P, T], F32, name="v1_pool", offset=0, align_bytes=64)
        kb_pool = keep.tile([P, T], F32, name="kb_pool")
        vs_pool = keep.tile([P, T], F32, name="vs_pool")
        gate_raw = [
            keep.tile([P, P], F32, name="gate_raw0"),
            keep.tile([P, P], F32, name="gate_raw1"),
        ]
        ident = keep.tile([P, P], F32, name="ident")

        nc.vector.memset(vs_pool[:], 0.0)
        nc.vector.memset(kb_pool[:KB_ROW, :], 0.0)
        k_rows = kT.rearrange("(p t) n -> p t n", t=PACK)
        for t in range(PACK):
            nc.sync.dma_start(out=k_pool[t][:], in_=k_rows[:, t, :])
            if t == 0:
                nc.sync.dma_start(offsets[:], offs)
                nc.sync.dma_start(out=kb_pool[KB_ROW:, :], in_=kb[0:1, :])
            if t == 1:
                nc.sync.dma_start(out=vs_pool[VS_ROW : VS_ROW + 1, :], in_=vs[0:1, :])
        nc.sync.dma_start(out=q_raw[:], in_=qT.rearrange("b (p t) q -> p (b t) q", t=PACK))
        nc.sync.dma_start(out=v0_pool[:], in_=vT[0:P, :])
        nc.sync.dma_start(out=v1_pool[:], in_=vT[P : 2 * P, :])
        og_rows = og.rearrange("b q e -> (b q) e")
        nc.sync.dma_start(out=gate_raw[0][:], in_=og_rows[:, :P])
        for a, b in ((0, 64), (64, 96), (96, P)):
            nc.sync.dma_start(out=gate_raw[1][a:b, :], in_=og_rows[a:b, P:])
        make_identity(nc, ident[:])

        k_grouped = keep.tile([P, N, PACK], BF16, name="k_grouped", align_bytes=64)
        k_low = keep.tile([P, 2, N], BF16, name="k_low")
        nc.vector.tensor_copy(k_low[:, 0, :], k_pool[0][:].indirect(offsets[:]))
        kb_row = keep.tile([P, N], F32, name="kb_row")
        nc.vector.tensor_copy(kb_row[:], kb_pool[:].indirect(offsets[:]))
        kb_turned = psum.tile([P, 4, P], F32, name="kb_turned", tag="bank_a")
        for c in range(4):
            nc.tensor.transpose(kb_turned[:, c, :], kb_row[:, c:N:PACK], ident[:])
        kb_cols = keep.tile([P, 4], F32, name="kb_cols")
        nc.scalar.copy(kb_cols[:], kb_turned[:, :, KB_ROW])
        kb_spread = psum.tile([P, 4, P], F32, name="kb_spread", tag="bank_b")
        for c in range(4):
            nc.tensor.transpose(kb_spread[:, c, :], kb_cols[:, c : c + 1].to_broadcast([P, P]), ident[:])
        order = (3, 0, 1, 2)
        first_kb = P + V0_SPLIT // PACK
        shared = keep.tile([P, first_kb + N], F32, name="shared", align_bytes=64)
        run = P // PACK

        def kb_piece(h):
            place = first_kb + P * ((h - order[-2]) % 4)
            return shared[:, place : place + P].rearrange("q (t s) -> q t s", t=PACK)

        nc.scalar.copy(kb_piece(0), kb_spread[:, :, :run])
        nc.scalar.copy(
            shared[:, first_kb : first_kb + 3 * P].rearrange("q (h t s) -> q h t s", h=3, t=PACK),
            kb_spread[:, :, run:].rearrange("q t (h s) -> q h t s", h=3),
        )

        nc.vector.tensor_copy(k_low[:, 1, :], k_pool[1][:].indirect(offsets[:]))
        nc.scalar.copy(k_grouped[:, :, 0:2], k_low[:].rearrange("p t n -> p n t"))
        vs_row = keep.tile([P, N], F32, name="vs_row")
        nc.vector.tensor_copy(vs_row[:], vs_pool[:].indirect(offsets[:]))
        vs_turned = psum.tile([P, PACK, P], F32, name="vs_turned", tag="bank_a")
        for t in range(PACK):
            nc.tensor.transpose(vs_turned[:, t, :], vs_row[:, t:N:PACK], ident[:])

        for t in (2, 3):
            nc.vector.tensor_copy(k_grouped[:, :K_SPLIT, t], k_pool[t][:].indirect(slots(0, K_SPLIT)))
            nc.scalar.activation(k_grouped[:, K_SPLIT:, t], k_pool[t][:].indirect(slots(K_SPLIT, N)), ACT.Copy)

        q_grouped = keep.tile([P, NQ, PACK], BF16, name="q_grouped", align_bytes=64)
        q_codes = keep.tile([P, NQ], U32, name="q_codes", align_bytes=64)
        q_scales = keep.tile([P, NQ], U8, name="q_scales", align_bytes=64)
        nc.scalar.copy(q_grouped[:], q_raw[:].rearrange("p t q -> p q t"))
        k_codes = [on_q.tile([P, P], U32, name="k_codes%d" % h, offset=512 * h, align_bytes=64) for h in range(3)]
        k_codes.append(keep.tile([P, P], U32, name="k_codes3", align_bytes=64))
        k_scales = keep.tile([P, N], U8, name="k_scales", align_bytes=64)
        k_flat = k_grouped[:].rearrange("p n t -> p (n t)")

        def quantize_keys(h):
            nc.vector.quantize_mx(
                out=k_codes[h][:].bitcast(FP8X4),
                scales=k_scales[:, h * P : (h + 1) * P],
                in_=k_flat[:, h * P * PACK : (h + 1) * P * PACK],
            )

        quantize_keys(order[0])
        nc.vector.quantize_mx(
            out=q_codes[:].bitcast(FP8X4), scales=q_scales[:], in_=q_grouped[:].rearrange("p q t -> p (q t)")
        )
        for h in order[1:]:
            quantize_keys(h)
        score_banks = ["bank_s0", "bank_s1", "bank_p", "bank_s2"]
        scores = [psum.tile([P, P], F32, name="scores%d" % h, tag=score_banks[h]) for h in range(N // P)]
        s = keep.tile([P, N], F32, name="s")
        for h in order:
            nc.tensor.matmul_mx(
                out=scores[h][:],
                lhsT=q_codes[:].bitcast(FP8X4),
                lhsT_scale=q_scales[:],
                rhs=k_codes[h][:].bitcast(FP8X4),
                rhs_scale=k_scales[:, h * P : (h + 1) * P],
                start=True,
                stop=True,
            )

        v0_dealt = shared[:, : N // 2].bitcast(BF16).rearrange("e (u s j) -> e s u j", u=2, j=2)
        v1_picked = on_picked.tile([P, N], BF16, name="v1_picked", offset=0, align_bytes=64)
        nc.scalar.activation(v0_dealt[:, : V0_SPLIT // PACK], v0_pool[:].indirect(slots(0, V0_SPLIT)), ACT.Copy)
        for h in order:
            nc.vector.tensor_tensor(
                s[:].rearrange("q (t s) -> q t s", t=PACK)[:, :, h * run : (h + 1) * run],
                kb_piece(h),
                scores[h][:].rearrange("q (s t) -> q t s", t=PACK),
                ADD,
            )
        neg_m = keep.tile([P, 1], F32, name="neg_m")
        nc.vector.tensor_reduce(neg_m[:], s[:], mybir.AxisListType.X, MAX, negate=True)
        nc.vector.tensor_copy(v0_dealt[:, V0_SPLIT // PACK :], v0_pool[:].indirect(slots(V0_SPLIT, N)))

        p = keep.tile([P, PACK, P], F32, name="p")
        part = keep.tile([P, PACK], F32, name="part")
        for t in range(PACK):
            nc.scalar.activation(
                p[:, t, :], s[:, t * P : (t + 1) * P], ACT.Exp, bias=neg_m[:], accum_out=part[:, t : t + 1]
            )
        vs_cols = s[:, 2 * P : 2 * P + PACK]
        nc.scalar.copy(vs_cols, vs_turned[:, :, VS_ROW])
        dealt = v1_picked[:].rearrange("e (u s j) -> e s u j", u=2, j=2)
        nc.vector.tensor_copy(dealt[:, : V1_SPLIT // PACK], v1_pool[:].indirect(slots(0, V1_SPLIT)))
        nc.scalar.activation(dealt[:, V1_SPLIT // PACK :], v1_pool[:].indirect(slots(V1_SPLIT, N)), ACT.Copy)

        p_turned = psum.tile([P, PACK, NQ], F32, name="p_turned", tag="bank_p")
        for t in range(PACK):
            nc.tensor.transpose(p_turned[:, t, :], p[:, t, :], ident[:])
        v0_turned = psum.tile([P, 2, P], F32, name="v0_turned", tag="bank_a")
        for u in range(2):
            nc.tensor.transpose(v0_turned[:, u, :], shared[:, u * P : (u + 1) * P], ident[:])
        v1_turned = psum.tile([P, 2, P], F32, name="v1_turned", tag="bank_v1")
        for u in range(2):
            nc.tensor.transpose(v1_turned[:, u, :], v1_picked[:].bitcast(F32)[:, u * P : (u + 1) * P], ident[:])

        gate_tanh = keep.tile([P, DV], F32, name="gate_tanh")
        nc.scalar.activation(gate_tanh[:, :P], gate_raw[0][:], ACT.Tanh, scale=0.5)
        nc.scalar.activation(gate_tanh[:, P:], gate_raw[1][:], ACT.Tanh, scale=0.5)
        total = on_v1.tile([P, 1], F32, name="total", offset=2048, align_bytes=64)
        nc.scalar.activation(part[:], part[:], ACT.Copy, accum_out=total[:])
        v_grouped = [
            on_v1.tile([P, N], BF16, name="v_grouped0", offset=1024, align_bytes=64),
            on_grouped.tile([P, N], BF16, name="v_grouped1", offset=0, align_bytes=64),
        ]
        pieces = ((0, 0, P), (1, 0, P // 2), (1, P // 2, P))
        for b, a, z in pieces:
            nc.scalar.copy(
                v_grouped[b][:].bitcast(F32).rearrange("s (e u) -> s e u", u=2)[:, a:z, :],
                (v0_turned, v1_turned)[b][:].rearrange("s u e -> s e u")[:, a:z, :],
            )
        gate = on_picked.tile([P, DV], F32, name="gate", offset=0, align_bytes=64)
        for b in range(2):
            cols = slice(b * P, (b + 1) * P)
            nc.scalar.activation(gate[:, cols], gate_tanh[:, cols], ACT.Copy, bias=0.5, scale=0.5)

        w = on_v1.tile([P, NQ, PACK], BF16, name="w", offset=0, align_bytes=64)
        w_codes = keep.tile([P, NQ], U32, name="w_codes", align_bytes=64)
        w_scales = keep.tile([P, NQ], U8, name="w_scales", align_bytes=64)
        q_halves = [slice(0, NQ // 2), slice(NQ // 2, NQ)]
        for rows in q_halves:
            nc.vector.tensor_tensor(
                w[:, rows, :],
                p_turned[:].rearrange("s t q -> s q t")[:, rows, :],
                vs_cols.unsqueeze(1).to_broadcast([P, NQ // 2, PACK]),
                MULT,
            )
        inv_total = keep.tile([P, 1], F32, name="inv_total")
        v_codes = [keep.tile([P, P], U32, name="v_codes%d" % b, align_bytes=64) for b in range(2)]
        v_scales = [keep.tile([P, P], U8, name="v_scales%d" % b, align_bytes=64) for b in range(2)]
        for rows in q_halves:
            nc.vector.quantize_mx(
                out=w_codes[:, rows].bitcast(FP8X4),
                scales=w_scales[:, rows],
                in_=w[:, rows, :].rearrange("p q t -> p (q t)"),
            )
            if rows.start == 0:
                nc.vector.reciprocal(inv_total[:], total[:])
        nc.vector.quantize_mx(out=v_codes[0][:].bitcast(FP8X4), scales=v_scales[0][:], in_=v_grouped[0][:])
        for b, a, z in pieces[1:]:
            nc.vector.quantize_mx(
                out=v_codes[b][:, a:z].bitcast(FP8X4),
                scales=v_scales[b][:, a:z],
                in_=v_grouped[b][:, a * PACK : z * PACK],
            )

        results = [
            on_grouped.tile([P, P], F32, name="result0", offset=0, align_bytes=64),
            keep.tile([P, P], F32, name="result1"),
        ]
        out_rows = out.rearrange("b q e -> (b q) e")
        y = []
        for (b, a, z), bank in zip(pieces, ("bank_y", "bank_b", "bank_s0")):
            acc = psum.tile([P, z - a], F32, name="y%d_%d" % (b, a), tag=bank)
            nc.tensor.matmul_mx(
                out=acc[:],
                lhsT=w_codes[:].bitcast(FP8X4),
                lhsT_scale=w_scales[:],
                rhs=v_codes[b][:, a:z].bitcast(FP8X4),
                rhs_scale=v_scales[b][:, a:z],
                start=True,
                stop=True,
            )
            y.append(acc)
        for (b, a, z), acc in zip(pieces, y):
            cols = slice(b * P + a, b * P + z)
            nc.vector.scalar_tensor_tensor(results[b][:, a:z], acc[:], inv_total[:], gate[:, cols], MULT, MULT)
            if z == P:
                nc.sync.dma_start(out=out_rows[:, b * P : (b + 1) * P], in_=results[b][:])
